import numpy as np
import ml_dtypes


def mxq(x, axis, fmt="e4m3"):
    dtype, down = {"e4m3": (ml_dtypes.float8_e4m3fn, 7), "e5m2": (ml_dtypes.float8_e5m2, 14)}[fmt]
    v = np.moveaxis(np.asarray(x, np.float32).astype(ml_dtypes.bfloat16).astype(np.float64), axis, -1)
    blocks = v.reshape(v.shape[:-1] + (-1, 32))
    amax = np.abs(blocks).max(-1, keepdims=True)
    byte = np.maximum(np.where(amax > 0, np.frexp(amax)[1] - 1 + 127, 0) - down, 1)
    scale = np.exp2(byte - 127.0)
    codes = (blocks / scale).astype(np.float32).astype(dtype).astype(np.float64)
    return np.moveaxis((codes * scale).reshape(v.shape), -1, axis)


WIDE = False


def mx_kscale(k):
    if not WIDE:
        return np.ones(k)
    levels = np.array([10, -10, 5, -5, 0])
    if k % 512:
        return np.exp2(np.random.permutation(np.resize(levels, k // 32))).repeat(32)
    a = np.empty((k // 512, 16))
    for p in range(k // 512):
        a[p, :8] = np.random.permutation(np.resize(levels, 8))
        for g in range(8):
            far = levels[np.abs(levels - a[p, g]) >= 10]
            a[p, g + 8] = far[np.random.randint(len(far))]
    return np.exp2(a.ravel()).repeat(32)


def f64(x):
    return np.asarray(x).astype(np.float64)


def striped(idx):
    return np.tile(idx.reshape(-1, 16).T, (8, 1)).astype(np.uint16)


def unstriped(offs):
    return offs[:16].T.reshape(-1).astype(np.int64)


E2M1 = np.array([0.0, 0.5, 1.0, 1.5, 2.0, 3.0, 4.0, 6.0, -0.0, -0.5, -1.0, -1.5, -2.0, -3.0, -4.0, -6.0])


def pack_weight(w, fmt):
    k, n = w.shape
    w = f64(np.asarray(w, np.float32).astype(ml_dtypes.bfloat16)).reshape(k // 32, 32, n)
    amax = np.abs(w).max(1)
    if fmt == "e4m3":
        byte = np.frexp(amax)[1] - 1 + 127 - 7
    else:
        mant, ex = np.frexp(amax / 6.0)
        byte = np.where(mant > 0.5, ex, ex - 1) + 127
    byte = np.clip(np.where(amax > 0, byte, 1), 1, 254)
    scaled = (w * np.exp2(127.0 - byte)[:, None, :]).reshape(k, n).astype(np.float32)
    by_word = np.ascontiguousarray(scaled.reshape(k // 512, 128, 4, n).transpose(0, 1, 3, 2))
    if fmt == "e4m3":
        words = by_word.astype(ml_dtypes.float8_e4m3fn).view(np.uint8)
    else:
        c = by_word.astype(ml_dtypes.float4_e2m1fn).view(np.uint8) & 0xF
        words = (c[..., 0::2] | (c[..., 1::2] << 4)).reshape(k // 512, 128, 2 * n)
    return np.ascontiguousarray(words), np.ascontiguousarray(byte.astype(np.uint8).reshape(k // 512, 16, n))


def unpack_weight(words, scales, fmt):
    g, _, n = scales.shape
    words = np.ascontiguousarray(words).reshape(g, 128, n, -1)
    if fmt == "e4m3":
        vals = words.view(ml_dtypes.float8_e4m3fn).astype(np.float64)
    else:
        nib = np.empty((g, 128, n, 4), np.uint8)
        nib[..., 0::2] = words & 0xF
        nib[..., 1::2] = words >> 4
        vals = E2M1[nib]
    vals = vals * np.repeat(np.exp2(scales.astype(np.float64) - 127.0), 8, axis=1)[..., None]
    return vals.transpose(0, 1, 3, 2).reshape(g * 512, n)


G, K, M, T, S = 2, 1024, 512, 2048, 512


def setup_inputs():
    n = np.random.standard_normal
    s = mx_kscale(K)[:, None]
    p_w4 = pack_weight(n((K, M)) / np.sqrt(K) / s, "e2m1")
    p_w8 = pack_weight(n((K, M)) / np.sqrt(K) / s, "e4m3")
    return {
        "xT": (n((K, T)) * s).astype(np.float32),
        "c": (n((K, S)) * s).astype(np.float32),
        "w4_words": p_w4[0],
        "w4_scales": p_w4[1],
        "w8_words": p_w8[0],
        "w8_scales": p_w8[1],
        "offs": striped(np.concatenate([np.random.permutation(T)[:S] for _ in range(G)])),
    }


def reference(xT, c, w4_words, w4_scales, w8_words, w8_scales, offs):
    idx = unstriped(offs).reshape(G, S)
    xm_ = mxq(np.max([f64(xT)[:, idx[g]] for g in range(G)], axis=0), 0, "e4m3")
    c_ = mxq(f64(c), 0, "e4m3")
    w4_ = unpack_weight(w4_words, w4_scales, "e2m1")
    w8_ = unpack_weight(w8_words, w8_scales, "e4m3")
    y = xm_.T @ w4_ + c_.T @ w8_
    return y

@@ -1,0 +1,173 @@
+from contextlib import ExitStack
+
+import concourse.mybir as mybir
+
+G, K, M, T, S = 2, 1024, 512, 2048, 512
+FLOPS = 2 * 2 * K * M * S
+
+F32 = mybir.dt.float32
+BF16 = mybir.dt.bfloat16
+I32 = mybir.dt.int32
+U32 = mybir.dt.uint32
+U16 = mybir.dt.uint16
+U8 = mybir.dt.uint8
+FP8X4 = mybir.dt.float8_e4m3fn_x4
+FP4X4 = mybir.dt.float4_e2m1fn_x4
+MAX = mybir.AluOpType.max
+
+P = 128
+PASSES = 2
+HALF_T = T // 2
+HALF_S = S // 2
+CHUNKS = {
+    (0, 0): [(0, 1024, 1024), (1024, 2048, 1376)],
+    (0, 1): [(0, 1024, 1024), (1024, 2048, 1376)],
+    (1, 0): [(0, 1024, 1024), (1024, 2048, 1376)],
+    (1, 1): [(0, 1024, 1024), (1024, 1536, 1024), (1536, 2048, 1696)],
+}
+
+
+def tile_list_sage_tm_none_kernel(tc, xT, c, w4_words, w4_scales, w8_words, w8_scales, offs, out):
+    nc = tc.nc
+    with ExitStack() as ctx:
+        keep = ctx.enter_context(tc.tile_pool(name="keep", bufs=1))
+        psum = ctx.enter_context(tc.psum_pool(name="psum", bufs=1))
+
+        offsets = keep.tile([P, G * S // 16], U16, name="offsets")
+        nc.sync.dma_start(offsets[:], offs)
+
+        w4 = keep.tile([P, PASSES, 2 * M], U8, name="w4", align_bytes=64)
+        w8 = keep.tile([P, PASSES, M], U32, name="w8", align_bytes=64)
+        s4 = keep.tile([P, PASSES, M], U8, name="s4", align_bytes=64)
+        s8 = keep.tile([P, PASSES, M], U8, name="s8", align_bytes=64)
+        nc.vector.memset(s4[:].bitcast(I32), 0)
+        nc.vector.memset(s8[:].bitcast(I32), 0)
+
+        def load_scales(plane, scales, q):
+            nc.sync.dma_start(
+                plane[32 * q : 32 * q + 4].bitcast(I32),
+                scales[:, 4 * q : 4 * q + 4, :].rearrange("a r n -> r a n").bitcast(I32),
+            )
+
+        x_rows = xT.rearrange("(a p i) t -> a p i t", a=PASSES, i=4)
+        c_rows = c.rearrange("(a p i) j -> a p i j", a=PASSES, i=4)
+        scale_loads = [(s4, w4_scales, q) for q in range(4)] + [(s8, w8_scales, q) for q in range(4)]
+
+        raw = {}
+
+        def load_x(a, u):
+            for t0, t1, split in CHUNKS[a, u]:
+                raw[a, u, t0] = keep.tile([P, 2, t1 - t0], F32, name="raw%d%d_%d" % (a, u, t0))
+                nc.sync.dma_start(raw[a, u, t0][:], x_rows[a, :, 2 * u : 2 * u + 2, t0:t1])
+                if scale_loads:
+                    load_scales(*scale_loads.pop(0))
+
+        c_raw = {}
+
+        def load_c(a, j0, j1):
+            c_raw[a, j0] = keep.tile([P, 4, j1 - j0], F32, name="c%d_%d" % (a, j0))
+            nc.sync.dma_start(c_raw[a, j0][:], c_rows[a, :, :, j0:j1])
+
+        load_x(0, 0)
+        load_x(0, 1)
+        load_x(1, 0)
+        load_x(1, 1)
+        nc.sync.dma_start(w4[:].bitcast(I32), w4_words.rearrange("a p b -> p a b").bitcast(I32))
+        load_c(0, 0, 256)
+        nc.sync.dma_start(w8[:].bitcast(I32), w8_words.rearrange("a p n i -> p a (n i)").bitcast(I32))
+        load_c(1, 0, 256)
+        load_c(0, 256, 512)
+        load_c(1, 256, 512)
+
+        picked = [keep.tile([P, 2, G, S], U32, name="picked%d" % a) for a in range(PASSES)]
+        acc = [psum.tile([P, M], F32, name="acc%d" % jt) for jt in range(4)]
+
+        def cast_pair(a, u):
+            table = keep.tile([P, T, 2], BF16, name="table%d%d" % (a, u))
+            for t0, t1, split in CHUNKS[a, u]:
+                rows = raw[a, u, t0][:].rearrange("p e t -> p t e")
+                if split > t0:
+                    nc.scalar.copy(table[:, t0:split], rows[:, 0 : split - t0])
+                if split < t1:
+                    nc.vector.tensor_copy(table[:, split:t1], rows[:, split - t0 : t1 - t0])
+            return table[:].rearrange("p t e -> p (t e)").bitcast(U32)
+
+        def gather_all(a, u, window):
+            nc.vector.tensor_copy(picked[a][:, u].rearrange("p g j -> p (g j)"), window.indirect(offsets[:]))
+
+        def gather_half(a, u, window, h, g):
+            col = (g * S + h * HALF_S) // 16
+            nc.vector.tensor_copy(
+                picked[a][:, u, g, h * HALF_S : (h + 1) * HALF_S],
+                window.indirect(offsets[:, col : col + HALF_S // 16]),
+            )
+
+        def maximum(a, j0, j1):
+            grouped = keep.tile([P, j1 - j0, 2, 2], BF16, name="xm%d_%d" % (a, j0), align_bytes=64)
+            pairs = picked[a][:].bitcast(BF16).rearrange("p u g (j e) -> p g j u e", e=2)
+            nc.vector.tensor_tensor(grouped[:], pairs[:, 0, j0:j1], pairs[:, 1, j0:j1], MAX)
+            return grouped[:].rearrange("p j u e -> p (j u e)")
+
+        def quantise(grouped, name):
+            width = grouped.shape[1] // 4
+            codes = keep.tile([P, width], U32, name="codes_" + name, align_bytes=64)
+            scales = keep.tile([P, width], U8, name="scales_" + name, align_bytes=64)
+            nc.vector.quantize_mx(out=codes[:].bitcast(FP8X4), scales=scales[:], in_=grouped)
+            return codes, scales
+
+        def multiply(quantised, jt0, weights, plane, start, stop):
+            codes, scales = quantised
+            for b in range(codes.shape[1] // P):
+                nc.tensor.matmul_mx(
+                    out=acc[jt0 + b][:],
+                    lhsT=codes[:, b * P : (b + 1) * P].bitcast(FP8X4),
+                    lhsT_scale=scales[:, b * P : (b + 1) * P],
+                    rhs=weights,
+                    rhs_scale=plane,
+                    start=start,
+                    stop=stop,
+                )
+
+        def group_c(rows, name, scalar_cols):
+            width = rows.shape[2]
+            grouped = keep.tile([P, width, 4], BF16, name="cg" + name, align_bytes=64)
+            src = rows.rearrange("p i j -> p j i")
+            nc.scalar.copy(grouped[:, 0:scalar_cols], src[:, 0:scalar_cols])
+            if scalar_cols < width:
+                nc.vector.tensor_copy(grouped[:, scalar_cols:width], src[:, scalar_cols:width])
+            return grouped[:].rearrange("p j i -> p (j i)")
+
+        w4_pass = [w4[:, a, :].bitcast(FP4X4) for a in range(PASSES)]
+        w8_pass = [w8[:, a, :].bitcast(FP8X4) for a in range(PASSES)]
+
+        def store(jt, copy):
+            result = keep.tile([P, M], F32, name="result%d" % jt)
+            copy(result[:], acc[jt][:])
+            nc.sync.dma_start(out[jt * P : (jt + 1) * P, :], result[:])
+
+        gather_all(0, 0, cast_pair(0, 0))
+        gather_all(0, 1, cast_pair(0, 1))
+        xm0 = maximum(0, 0, S)
+        multiply(quantise(xm0, "x0"), 0, w4_pass[0], s4[:, 0, :], True, False)
+        gather_all(1, 0, cast_pair(1, 0))
+        window = cast_pair(1, 1)
+        gather_half(1, 1, window, 0, 0)
+        gather_half(1, 1, window, 0, 1)
+        gather_half(1, 1, window, 1, 0)
+        xm1 = maximum(1, 0, HALF_S)
+        gather_half(1, 1, window, 1, 1)
+        cg = group_c(c_raw[0, 0][:], "00", HALF_S)
+        multiply(quantise(xm1, "x10"), 0, w4_pass[1], s4[:, 1, :], False, False)
+        multiply(quantise(cg, "c00"), 0, w8_pass[0], s8[:, 0, :], False, False)
+        xm1 = maximum(1, HALF_S, S)
+        cg = group_c(c_raw[1, 0][:], "10", HALF_S)
+        multiply(quantise(cg, "c10"), 0, w8_pass[1], s8[:, 1, :], False, True)
+        multiply(quantise(xm1, "x11"), 2, w4_pass[1], s4[:, 1, :], False, False)
+        cg0 = group_c(c_raw[0, 256][:], "01", 128)
+        store(0, nc.scalar.copy)
+        cg1 = group_c(c_raw[1, 256][:], "11", 80)
+        store(1, nc.scalar.copy)
+        multiply(quantise(cg0, "c01"), 2, w8_pass[0], s8[:, 0, :], False, False)
+        multiply(quantise(cg1, "c11"), 2, w8_pass[1], s8[:, 1, :], False, True)
+        store(2, nc.scalar.copy)
+        store(3, nc.vector.tensor_copy)

@@ -21,9 +21,9 @@ HALF_T = T // 2
 HALF_S = S // 2
 CHUNKS = {
     (0, 0): [(0, 1024, 1024), (1024, 2048, 1376)],
-    (0, 1): [(0, 1024, 1024), (1024, 2048, 1376)],
-    (1, 0): [(0, 1024, 1024), (1024, 2048, 1376)],
-    (1, 1): [(0, 1024, 1024), (1024, 1536, 1024), (1536, 2048, 1696)],
+    (0, 1): [(1024, 2048, 2048), (0, 1024, 352)],
+    (1, 0): [(0, 1024, 1024), (1024, 2048, 1632)],
+    (1, 1): [(1024, 2048, 2048), (0, 512, 0), (512, 1024, 768)],
 }
 
 
@@ -34,7 +34,6 @@ def tile_list_sage_tm_none_kernel(tc, xT, c, w4_words, w4_scales, w8_words, w8_s
         psum = ctx.enter_context(tc.psum_pool(name="psum", bufs=1))
 
         offsets = keep.tile([P, G * S // 16], U16, name="offsets")
-        nc.sync.dma_start(offsets[:], offs)
 
         w4 = keep.tile([P, PASSES, 2 * M], U8, name="w4", align_bytes=64)
         w8 = keep.tile([P, PASSES, M], U32, name="w8", align_bytes=64)
@@ -44,7 +43,7 @@ def tile_list_sage_tm_none_kernel(tc, xT, c, w4_words, w4_scales, w8_words, w8_s
         nc.vector.memset(s8[:].bitcast(I32), 0)
 
         def load_scales(plane, scales, q):
-            nc.sync.dma_start(
+            nc.gpsimd.dma_start(
                 plane[32 * q : 32 * q + 4].bitcast(I32),
                 scales[:, 4 * q : 4 * q + 4, :].rearrange("a r n -> r a n").bitcast(I32),
             )
@@ -53,14 +52,15 @@ def tile_list_sage_tm_none_kernel(tc, xT, c, w4_words, w4_scales, w8_words, w8_s
         c_rows = c.rearrange("(a p i) j -> a p i j", a=PASSES, i=4)
         scale_loads = [(s4, w4_scales, q) for q in range(4)] + [(s8, w8_scales, q) for q in range(4)]
 
+        for plane, scales, q in scale_loads:
+            load_scales(plane, scales, q)
+
         raw = {}
 
         def load_x(a, u):
             for t0, t1, split in CHUNKS[a, u]:
                 raw[a, u, t0] = keep.tile([P, 2, t1 - t0], F32, name="raw%d%d_%d" % (a, u, t0))
                 nc.sync.dma_start(raw[a, u, t0][:], x_rows[a, :, 2 * u : 2 * u + 2, t0:t1])
-                if scale_loads:
-                    load_scales(*scale_loads.pop(0))
 
         c_raw = {}
 
@@ -69,28 +69,32 @@ def tile_list_sage_tm_none_kernel(tc, xT, c, w4_words, w4_scales, w8_words, w8_s
             nc.sync.dma_start(c_raw[a, j0][:], c_rows[a, :, :, j0:j1])
 
         load_x(0, 0)
+        nc.sync.dma_start(offsets[:], offs)
         load_x(0, 1)
         load_x(1, 0)
         load_x(1, 1)
-        nc.sync.dma_start(w4[:].bitcast(I32), w4_words.rearrange("a p b -> p a b").bitcast(I32))
         load_c(0, 0, 256)
-        nc.sync.dma_start(w8[:].bitcast(I32), w8_words.rearrange("a p n i -> p a (n i)").bitcast(I32))
+        nc.sync.dma_start(w4[:].bitcast(I32), w4_words.rearrange("a p b -> p a b").bitcast(I32))
+        nc.sync.dma_start(w8[:, 0].bitcast(I32), w8_words[0].rearrange("p n i -> p (n i)").bitcast(I32))
         load_c(1, 0, 256)
         load_c(0, 256, 512)
         load_c(1, 256, 512)
+        nc.sync.dma_start(w8[:, 1].bitcast(I32), w8_words[1].rearrange("p n i -> p (n i)").bitcast(I32))
 
         picked = [keep.tile([P, 2, G, S], U32, name="picked%d" % a) for a in range(PASSES)]
         acc = [psum.tile([P, M], F32, name="acc%d" % jt) for jt in range(4)]
 
+        ring = keep.tile([P, T + HALF_T, 2], BF16, name="ring")
+
         def cast_pair(a, u):
-            table = keep.tile([P, T, 2], BF16, name="table%d%d" % (a, u))
+            table = ring[:, u * HALF_T : u * HALF_T + T]
             for t0, t1, split in CHUNKS[a, u]:
                 rows = raw[a, u, t0][:].rearrange("p e t -> p t e")
                 if split > t0:
                     nc.scalar.copy(table[:, t0:split], rows[:, 0 : split - t0])
                 if split < t1:
                     nc.vector.tensor_copy(table[:, split:t1], rows[:, split - t0 : t1 - t0])
-            return table[:].rearrange("p t e -> p (t e)").bitcast(U32)
+            return table.rearrange("p t e -> p (t e)").bitcast(U32)
 
         def gather_all(a, u, window):
             nc.vector.tensor_copy(picked[a][:, u].rearrange("p g j -> p (g j)"), window.indirect(offsets[:]))
@@ -140,34 +144,34 @@ def tile_list_sage_tm_none_kernel(tc, xT, c, w4_words, w4_scales, w8_words, w8_s
         w4_pass = [w4[:, a, :].bitcast(FP4X4) for a in range(PASSES)]
         w8_pass = [w8[:, a, :].bitcast(FP8X4) for a in range(PASSES)]
 
-        def store(jt, copy):
-            result = keep.tile([P, M], F32, name="result%d" % jt)
-            copy(result[:], acc[jt][:])
-            nc.sync.dma_start(out[jt * P : (jt + 1) * P, :], result[:])
+        def store(jt, copy, result):
+            copy(result, acc[jt][:])
+            nc.sync.dma_start(out[jt * P : (jt + 1) * P, :], result)
 
-        gather_all(0, 0, cast_pair(0, 0))
-        gather_all(0, 1, cast_pair(0, 1))
-        xm0 = maximum(0, 0, S)
-        multiply(quantise(xm0, "x0"), 0, w4_pass[0], s4[:, 0, :], True, False)
-        gather_all(1, 0, cast_pair(1, 0))
-        window = cast_pair(1, 1)
-        gather_half(1, 1, window, 0, 0)
-        gather_half(1, 1, window, 0, 1)
-        gather_half(1, 1, window, 1, 0)
-        xm1 = maximum(1, 0, HALF_S)
-        gather_half(1, 1, window, 1, 1)
-        cg = group_c(c_raw[0, 0][:], "00", HALF_S)
-        multiply(quantise(xm1, "x10"), 0, w4_pass[1], s4[:, 1, :], False, False)
-        multiply(quantise(cg, "c00"), 0, w8_pass[0], s8[:, 0, :], False, False)
-        xm1 = maximum(1, HALF_S, S)
-        cg = group_c(c_raw[1, 0][:], "10", HALF_S)
-        multiply(quantise(cg, "c10"), 0, w8_pass[1], s8[:, 1, :], False, True)
-        multiply(quantise(xm1, "x11"), 2, w4_pass[1], s4[:, 1, :], False, False)
-        cg0 = group_c(c_raw[0, 256][:], "01", 128)
-        store(0, nc.scalar.copy)
-        cg1 = group_c(c_raw[1, 256][:], "11", 80)
-        store(1, nc.scalar.copy)
-        multiply(quantise(cg0, "c01"), 2, w8_pass[0], s8[:, 0, :], False, False)
-        multiply(quantise(cg1, "c11"), 2, w8_pass[1], s8[:, 1, :], False, True)
-        store(2, nc.scalar.copy)
-        store(3, nc.vector.tensor_copy)
+        def neighbours(a):
+            gather_all(a, 0, cast_pair(a, 0))
+            window = cast_pair(a, 1)
+            gather_half(a, 1, window, 0, 0)
+            gather_half(a, 1, window, 0, 1)
+            gather_half(a, 1, window, 1, 0)
+            low = maximum(a, 0, HALF_S)
+            gather_half(a, 1, window, 1, 1)
+            return low
+
+        low = neighbours(0)
+        multiply(quantise(low, "x00"), 0, w4_pass[0], s4[:, 0, :], True, False)
+        multiply(quantise(maximum(0, HALF_S, S), "x01"), 2, w4_pass[0], s4[:, 0, :], True, False)
+        low = neighbours(1)
+        cg = {key: group_c(c_raw[key][:], "%d_%d" % key, HALF_S) for key in [(0, 0), (1, 0), (0, 256), (1, 256)]}
+        multiply(quantise(low, "x10"), 0, w4_pass[1], s4[:, 1, :], False, False)
+        multiply(quantise(cg[0, 0], "c00"), 0, w8_pass[0], s8[:, 0, :], False, False)
+        multiply(quantise(cg[1, 0], "c10"), 0, w8_pass[1], s8[:, 1, :], False, True)
+        high = maximum(1, HALF_S, S)
+        multiply(quantise(cg[0, 256], "c01"), 2, w8_pass[0], s8[:, 0, :], False, False)
+        multiply(quantise(high, "x11"), 2, w4_pass[1], s4[:, 1, :], False, False)
+        multiply(quantise(cg[1, 256], "c11"), 2, w8_pass[1], s8[:, 1, :], False, True)
+        spent = [c_raw[a, 256][:].rearrange("p (b i) j -> p b (i j)", b=2) for a in range(PASSES)]
+        store(0, nc.scalar.copy, spent[1][:, 0])
+        store(1, nc.scalar.copy, spent[1][:, 1])
+        store(2, nc.vector.tensor_copy, spent[0][:, 0])
+        store(3, nc.scalar.copy, spent[0][:, 1])

@@ -21,7 +21,7 @@ HALF_T = T // 2
 HALF_S = S // 2
 CHUNKS = {
     (0, 0): [(0, 1024, 1024), (1024, 2048, 1376)],
-    (0, 1): [(1024, 2048, 2048), (0, 1024, 352)],
+    (0, 1): [(1024, 2048, 2048), (0, 512, 0), (512, 1024, 672)],
     (1, 0): [(0, 1024, 1024), (1024, 2048, 1632)],
     (1, 1): [(1024, 2048, 2048), (0, 512, 0), (512, 1024, 768)],
 }
@@ -75,25 +75,27 @@ def tile_list_sage_tm_none_kernel(tc, xT, c, w4_words, w4_scales, w8_words, w8_s
         load_x(1, 1)
         load_c(0, 0, 256)
         nc.sync.dma_start(w4[:].bitcast(I32), w4_words.rearrange("a p b -> p a b").bitcast(I32))
-        nc.sync.dma_start(w8[:, 0].bitcast(I32), w8_words[0].rearrange("p n i -> p (n i)").bitcast(I32))
+        nc.sync.dma_start(w8[:].bitcast(I32), w8_words.rearrange("a p n i -> p a (n i)").bitcast(I32))
         load_c(1, 0, 256)
         load_c(0, 256, 512)
         load_c(1, 256, 512)
-        nc.sync.dma_start(w8[:, 1].bitcast(I32), w8_words[1].rearrange("p n i -> p (n i)").bitcast(I32))
 
         picked = [keep.tile([P, 2, G, S], U32, name="picked%d" % a) for a in range(PASSES)]
         acc = [psum.tile([P, M], F32, name="acc%d" % jt) for jt in range(4)]
 
         ring = keep.tile([P, T + HALF_T, 2], BF16, name="ring")
 
+        def interleave(copy, grouped, rows):
+            copy(grouped.rearrange("p (b t) e -> p b e t", t=4), rows.rearrange("p e (b t) -> p b e t", t=4))
+
         def cast_pair(a, u):
             table = ring[:, u * HALF_T : u * HALF_T + T]
             for t0, t1, split in CHUNKS[a, u]:
-                rows = raw[a, u, t0][:].rearrange("p e t -> p t e")
+                rows = raw[a, u, t0]
                 if split > t0:
-                    nc.scalar.copy(table[:, t0:split], rows[:, 0 : split - t0])
+                    interleave(nc.scalar.copy, table[:, t0:split], rows[:, :, 0 : split - t0])
                 if split < t1:
-                    nc.vector.tensor_copy(table[:, split:t1], rows[:, split - t0 : t1 - t0])
+                    interleave(nc.vector.tensor_copy, table[:, split:t1], rows[:, :, split - t0 : t1 - t0])
             return table.rearrange("p t e -> p (t e)").bitcast(U32)
 
         def gather_all(a, u, window):
@@ -106,11 +108,16 @@ def tile_list_sage_tm_none_kernel(tc, xT, c, w4_words, w4_scales, w8_words, w8_s
                 window.indirect(offsets[:, col : col + HALF_S // 16]),
             )
 
-        def maximum(a, j0, j1):
-            grouped = keep.tile([P, j1 - j0, 2, 2], BF16, name="xm%d_%d" % (a, j0), align_bytes=64)
+        def maximum(a, h, grouped):
             pairs = picked[a][:].bitcast(BF16).rearrange("p u g (j e) -> p g j u e", e=2)
-            nc.vector.tensor_tensor(grouped[:], pairs[:, 0, j0:j1], pairs[:, 1, j0:j1], MAX)
-            return grouped[:].rearrange("p j u e -> p (j u e)")
+            cols = slice(h * HALF_S, (h + 1) * HALF_S)
+            nc.vector.tensor_tensor(
+                grouped.rearrange("p (j u e) -> p j u e", u=2, e=2), pairs[:, 0, cols], pairs[:, 1, cols], MAX
+            )
+            return grouped
+
+        def fresh(name):
+            return keep.tile([P, 4 * HALF_S], BF16, name=name, align_bytes=64)[:]
 
         def quantise(grouped, name):
             width = grouped.shape[1] // 4
@@ -132,13 +139,9 @@ def tile_list_sage_tm_none_kernel(tc, xT, c, w4_words, w4_scales, w8_words, w8_s
                     stop=stop,
                 )
 
-        def group_c(rows, name, scalar_cols):
-            width = rows.shape[2]
-            grouped = keep.tile([P, width, 4], BF16, name="cg" + name, align_bytes=64)
-            src = rows.rearrange("p i j -> p j i")
-            nc.scalar.copy(grouped[:, 0:scalar_cols], src[:, 0:scalar_cols])
-            if scalar_cols < width:
-                nc.vector.tensor_copy(grouped[:, scalar_cols:width], src[:, scalar_cols:width])
+        def group_c(rows, name):
+            grouped = keep.tile([P, HALF_S, 4], BF16, name="cg" + name, align_bytes=64)
+            interleave(nc.scalar.copy, grouped[:], rows)
             return grouped[:].rearrange("p j i -> p (j i)")
 
         w4_pass = [w4[:, a, :].bitcast(FP4X4) for a in range(PASSES)]
@@ -154,19 +157,19 @@ def tile_list_sage_tm_none_kernel(tc, xT, c, w4_words, w4_scales, w8_words, w8_s
             gather_half(a, 1, window, 0, 0)
             gather_half(a, 1, window, 0, 1)
             gather_half(a, 1, window, 1, 0)
-            low = maximum(a, 0, HALF_S)
+            low = maximum(a, 0, fresh("low%d" % a))
             gather_half(a, 1, window, 1, 1)
             return low
 
         low = neighbours(0)
         multiply(quantise(low, "x00"), 0, w4_pass[0], s4[:, 0, :], True, False)
-        multiply(quantise(maximum(0, HALF_S, S), "x01"), 2, w4_pass[0], s4[:, 0, :], True, False)
+        multiply(quantise(maximum(0, 1, fresh("high0")), "x01"), 2, w4_pass[0], s4[:, 0, :], True, False)
         low = neighbours(1)
-        cg = {key: group_c(c_raw[key][:], "%d_%d" % key, HALF_S) for key in [(0, 0), (1, 0), (0, 256), (1, 256)]}
+        cg = {key: group_c(c_raw[key][:], "%d_%d" % key) for key in [(0, 0), (1, 0), (0, 256), (1, 256)]}
         multiply(quantise(low, "x10"), 0, w4_pass[1], s4[:, 1, :], False, False)
         multiply(quantise(cg[0, 0], "c00"), 0, w8_pass[0], s8[:, 0, :], False, False)
         multiply(quantise(cg[1, 0], "c10"), 0, w8_pass[1], s8[:, 1, :], False, True)
-        high = maximum(1, HALF_S, S)
+        high = maximum(1, 1, cg[1, 0])
         multiply(quantise(cg[0, 256], "c01"), 2, w8_pass[0], s8[:, 0, :], False, False)
         multiply(quantise(high, "x11"), 2, w4_pass[1], s4[:, 1, :], False, False)
         multiply(quantise(cg[1, 256], "c11"), 2, w8_pass[1], s8[:, 1, :], False, True)

@@ -20,10 +20,10 @@ PASSES = 2
 HALF_T = T // 2
 HALF_S = S // 2
 CHUNKS = {
-    (0, 0): [(0, 1024, 1024), (1024, 2048, 1376)],
-    (0, 1): [(1024, 2048, 2048), (0, 512, 0), (512, 1024, 672)],
+    (0, 0): [(0, 2048, 688)],
+    (0, 1): [(1024, 2048, 2048), (0, 1024, 352)],
     (1, 0): [(0, 1024, 1024), (1024, 2048, 1632)],
-    (1, 1): [(1024, 2048, 2048), (0, 512, 0), (512, 1024, 768)],
+    (1, 1): [(1024, 2048, 2048), (0, 512, 0), (512, 1024, 672)],
 }
 
 
@@ -73,12 +73,11 @@ def tile_list_sage_tm_none_kernel(tc, xT, c, w4_words, w4_scales, w8_words, w8_s
         load_x(0, 1)
         load_x(1, 0)
         load_x(1, 1)
-        load_c(0, 0, 256)
+        load_c(0, 0, 512)
         nc.sync.dma_start(w4[:].bitcast(I32), w4_words.rearrange("a p b -> p a b").bitcast(I32))
-        nc.sync.dma_start(w8[:].bitcast(I32), w8_words.rearrange("a p n i -> p a (n i)").bitcast(I32))
-        load_c(1, 0, 256)
-        load_c(0, 256, 512)
-        load_c(1, 256, 512)
+        load_c(1, 0, 512)
+        nc.sync.dma_start(w8[:, 0].bitcast(I32), w8_words[0].rearrange("p n i -> p (n i)").bitcast(I32))
+        nc.sync.dma_start(w8[:, 1].bitcast(I32), w8_words[1].rearrange("p n i -> p (n i)").bitcast(I32))
 
         picked = [keep.tile([P, 2, G, S], U32, name="picked%d" % a) for a in range(PASSES)]
         acc = [psum.tile([P, M], F32, name="acc%d" % jt) for jt in range(4)]
@@ -139,15 +138,19 @@ def tile_list_sage_tm_none_kernel(tc, xT, c, w4_words, w4_scales, w8_words, w8_s
                     stop=stop,
                 )
 
-        def group_c(rows, name):
-            grouped = keep.tile([P, HALF_S, 4], BF16, name="cg" + name, align_bytes=64)
-            interleave(nc.scalar.copy, grouped[:], rows)
+        def group_c(a, h, scalar_cols):
+            grouped = keep.tile([P, HALF_S, 4], BF16, name="cg%d%d" % (a, h), align_bytes=64)
+            rows = c_raw[a, 0][:, :, h * HALF_S : (h + 1) * HALF_S]
+            interleave(nc.scalar.copy, grouped[:, 0:scalar_cols], rows[:, :, 0:scalar_cols])
+            if scalar_cols < HALF_S:
+                interleave(nc.vector.tensor_copy, grouped[:, scalar_cols:HALF_S], rows[:, :, scalar_cols:HALF_S])
             return grouped[:].rearrange("p j i -> p (j i)")
 
         w4_pass = [w4[:, a, :].bitcast(FP4X4) for a in range(PASSES)]
         w8_pass = [w8[:, a, :].bitcast(FP8X4) for a in range(PASSES)]
 
-        def store(jt, copy, result):
+        def store(jt, copy):
+            result = keep.tile([P, M], F32, name="result%d" % jt)[:]
             copy(result, acc[jt][:])
             nc.sync.dma_start(out[jt * P : (jt + 1) * P, :], result)
 
@@ -165,16 +168,20 @@ def tile_list_sage_tm_none_kernel(tc, xT, c, w4_words, w4_scales, w8_words, w8_s
         multiply(quantise(low, "x00"), 0, w4_pass[0], s4[:, 0, :], True, False)
         multiply(quantise(maximum(0, 1, fresh("high0")), "x01"), 2, w4_pass[0], s4[:, 0, :], True, False)
         low = neighbours(1)
-        cg = {key: group_c(c_raw[key][:], "%d_%d" % key) for key in [(0, 0), (1, 0), (0, 256), (1, 256)]}
-        multiply(quantise(low, "x10"), 0, w4_pass[1], s4[:, 1, :], False, False)
-        multiply(quantise(cg[0, 0], "c00"), 0, w8_pass[0], s8[:, 0, :], False, False)
-        multiply(quantise(cg[1, 0], "c10"), 0, w8_pass[1], s8[:, 1, :], False, True)
-        high = maximum(1, 1, cg[1, 0])
-        multiply(quantise(cg[0, 256], "c01"), 2, w8_pass[0], s8[:, 0, :], False, False)
-        multiply(quantise(high, "x11"), 2, w4_pass[1], s4[:, 1, :], False, False)
-        multiply(quantise(cg[1, 256], "c11"), 2, w8_pass[1], s8[:, 1, :], False, True)
-        spent = [c_raw[a, 256][:].rearrange("p (b i) j -> p b (i j)", b=2) for a in range(PASSES)]
-        store(0, nc.scalar.copy, spent[1][:, 0])
-        store(1, nc.scalar.copy, spent[1][:, 1])
-        store(2, nc.vector.tensor_copy, spent[0][:, 0])
-        store(3, nc.scalar.copy, spent[0][:, 1])
+        x10 = quantise(low, "x10")
+        c00 = quantise(group_c(0, 0, HALF_S), "c00")
+        high = maximum(1, 1, fresh("high1"))
+        c01 = quantise(group_c(0, 1, HALF_S), "c01")
+        x11 = quantise(high, "x11")
+        c10 = quantise(group_c(1, 0, HALF_S), "c10")
+        c11 = quantise(group_c(1, 1, 128), "c11")
+        multiply(x10, 0, w4_pass[1], s4[:, 1, :], False, False)
+        multiply(c00, 0, w8_pass[0], s8[:, 0, :], False, False)
+        multiply(c10, 0, w8_pass[1], s8[:, 1, :], False, True)
+        multiply(c01, 2, w8_pass[0], s8[:, 0, :], False, False)
+        multiply(x11, 2, w4_pass[1], s4[:, 1, :], False, False)
+        multiply(c11, 2, w8_pass[1], s8[:, 1, :], False, True)
+        store(0, nc.scalar.copy)
+        store(1, nc.scalar.copy)
+        store(2, nc.vector.tensor_copy)
+        store(3, nc.scalar.copy)

@@ -17,13 +17,12 @@ MAX = mybir.AluOpType.max
 
 P = 128
 PASSES = 2
-HALF_T = T // 2
 HALF_S = S // 2
 CHUNKS = {
-    (0, 0): [(0, 2048, 688)],
-    (0, 1): [(1024, 2048, 2048), (0, 1024, 352)],
-    (1, 0): [(0, 1024, 1024), (1024, 2048, 1632)],
-    (1, 1): [(1024, 2048, 2048), (0, 512, 0), (512, 1024, 672)],
+    (0, 0): [(0, 1024, 512), (1024, 2048, 1376)],
+    (0, 1): [(0, 1024, 896), (1024, 2048, 1376)],
+    (1, 0): [(0, 1024, 1024), (1024, 2048, 1792)],
+    (1, 1): [(0, 1024, 1024), (1024, 1536, 1024), (1536, 2048, 1824)],
 }
 
 
@@ -42,18 +41,15 @@ def tile_list_sage_tm_none_kernel(tc, xT, c, w4_words, w4_scales, w8_words, w8_s
         nc.vector.memset(s4[:].bitcast(I32), 0)
         nc.vector.memset(s8[:].bitcast(I32), 0)
 
-        def load_scales(plane, scales, q):
-            nc.gpsimd.dma_start(
-                plane[32 * q : 32 * q + 4].bitcast(I32),
-                scales[:, 4 * q : 4 * q + 4, :].rearrange("a r n -> r a n").bitcast(I32),
-            )
+        for plane, scales in ((s4, w4_scales), (s8, w8_scales)):
+            for q in range(4):
+                nc.gpsimd.dma_start(
+                    plane[32 * q : 32 * q + 4].bitcast(I32),
+                    scales[:, 4 * q : 4 * q + 4, :].rearrange("a r n -> r a n").bitcast(I32),
+                )
 
         x_rows = xT.rearrange("(a p i) t -> a p i t", a=PASSES, i=4)
         c_rows = c.rearrange("(a p i) j -> a p i j", a=PASSES, i=4)
-        scale_loads = [(s4, w4_scales, q) for q in range(4)] + [(s8, w8_scales, q) for q in range(4)]
-
-        for plane, scales, q in scale_loads:
-            load_scales(plane, scales, q)
 
         raw = {}
 
@@ -62,88 +58,67 @@ def tile_list_sage_tm_none_kernel(tc, xT, c, w4_words, w4_scales, w8_words, w8_s
                 raw[a, u, t0] = keep.tile([P, 2, t1 - t0], F32, name="raw%d%d_%d" % (a, u, t0))
                 nc.sync.dma_start(raw[a, u, t0][:], x_rows[a, :, 2 * u : 2 * u + 2, t0:t1])
 
-        c_raw = {}
-
-        def load_c(a, j0, j1):
-            c_raw[a, j0] = keep.tile([P, 4, j1 - j0], F32, name="c%d_%d" % (a, j0))
-            nc.sync.dma_start(c_raw[a, j0][:], c_rows[a, :, :, j0:j1])
+        c_raw = [keep.tile([P, 4, S], F32, name="c%d" % a) for a in range(PASSES)]
 
         load_x(0, 0)
         nc.sync.dma_start(offsets[:], offs)
         load_x(0, 1)
         load_x(1, 0)
         load_x(1, 1)
-        load_c(0, 0, 512)
-        nc.sync.dma_start(w4[:].bitcast(I32), w4_words.rearrange("a p b -> p a b").bitcast(I32))
-        load_c(1, 0, 512)
-        nc.sync.dma_start(w8[:, 0].bitcast(I32), w8_words[0].rearrange("p n i -> p (n i)").bitcast(I32))
-        nc.sync.dma_start(w8[:, 1].bitcast(I32), w8_words[1].rearrange("p n i -> p (n i)").bitcast(I32))
+        nc.sync.dma_start(c_raw[0][:], c_rows[0])
+        nc.sync.dma_start(w4[:, 0].bitcast(I32), w4_words[0].bitcast(I32))
+        nc.sync.dma_start(c_raw[1][:], c_rows[1])
+        nc.sync.dma_start(w4[:, 1].bitcast(I32), w4_words[1].bitcast(I32))
+        nc.sync.dma_start(w8[:].bitcast(I32), w8_words.rearrange("a p n i -> p a (n i)").bitcast(I32))
 
         picked = [keep.tile([P, 2, G, S], U32, name="picked%d" % a) for a in range(PASSES)]
         acc = [psum.tile([P, M], F32, name="acc%d" % jt) for jt in range(4)]
 
-        ring = keep.tile([P, T + HALF_T, 2], BF16, name="ring")
-
         def interleave(copy, grouped, rows):
             copy(grouped.rearrange("p (b t) e -> p b e t", t=4), rows.rearrange("p e (b t) -> p b e t", t=4))
 
-        def cast_pair(a, u):
-            table = ring[:, u * HALF_T : u * HALF_T + T]
+        def gather_pair(a, u):
+            table = keep.tile([P, T, 2], BF16, name="table%d%d" % (a, u))
             for t0, t1, split in CHUNKS[a, u]:
                 rows = raw[a, u, t0]
                 if split > t0:
                     interleave(nc.scalar.copy, table[:, t0:split], rows[:, :, 0 : split - t0])
                 if split < t1:
                     interleave(nc.vector.tensor_copy, table[:, split:t1], rows[:, :, split - t0 : t1 - t0])
-            return table.rearrange("p t e -> p (t e)").bitcast(U32)
-
-        def gather_all(a, u, window):
+            window = table[:].rearrange("p t e -> p (t e)").bitcast(U32)
             nc.vector.tensor_copy(picked[a][:, u].rearrange("p g j -> p (g j)"), window.indirect(offsets[:]))
 
-        def gather_half(a, u, window, h, g):
-            col = (g * S + h * HALF_S) // 16
-            nc.vector.tensor_copy(
-                picked[a][:, u, g, h * HALF_S : (h + 1) * HALF_S],
-                window.indirect(offsets[:, col : col + HALF_S // 16]),
-            )
-
-        def maximum(a, h, grouped):
+        def maximum(a, j0, width):
+            grouped = keep.tile([P, 4 * width], BF16, name="xm%d_%d" % (a, j0), align_bytes=64)
             pairs = picked[a][:].bitcast(BF16).rearrange("p u g (j e) -> p g j u e", e=2)
-            cols = slice(h * HALF_S, (h + 1) * HALF_S)
+            cols = slice(j0, j0 + width)
             nc.vector.tensor_tensor(
-                grouped.rearrange("p (j u e) -> p j u e", u=2, e=2), pairs[:, 0, cols], pairs[:, 1, cols], MAX
+                grouped[:].rearrange("p (j u e) -> p j u e", u=2, e=2), pairs[:, 0, cols], pairs[:, 1, cols], MAX
             )
-            return grouped
-
-        def fresh(name):
-            return keep.tile([P, 4 * HALF_S], BF16, name=name, align_bytes=64)[:]
+            return grouped[:]
 
         def quantise(grouped, name):
             width = grouped.shape[1] // 4
             codes = keep.tile([P, width], U32, name="codes_" + name, align_bytes=64)
             scales = keep.tile([P, width], U8, name="scales_" + name, align_bytes=64)
             nc.vector.quantize_mx(out=codes[:].bitcast(FP8X4), scales=scales[:], in_=grouped)
-            return codes, scales
+            return [(codes[:, b * P : (b + 1) * P], scales[:, b * P : (b + 1) * P]) for b in range(width // P)]
 
-        def multiply(quantised, jt0, weights, plane, start, stop):
-            codes, scales = quantised
-            for b in range(codes.shape[1] // P):
-                nc.tensor.matmul_mx(
-                    out=acc[jt0 + b][:],
-                    lhsT=codes[:, b * P : (b + 1) * P].bitcast(FP8X4),
-                    lhsT_scale=scales[:, b * P : (b + 1) * P],
-                    rhs=weights,
-                    rhs_scale=plane,
-                    start=start,
-                    stop=stop,
-                )
+        def multiply(jt, operand, weights, plane, start, stop):
+            codes, scales = operand
+            nc.tensor.matmul_mx(
+                out=acc[jt][:],
+                lhsT=codes.bitcast(FP8X4),
+                lhsT_scale=scales,
+                rhs=weights,
+                rhs_scale=plane,
+                start=start,
+                stop=stop,
+            )
 
-        def group_c(a, h, scalar_cols):
-            grouped = keep.tile([P, HALF_S, 4], BF16, name="cg%d%d" % (a, h), align_bytes=64)
-            rows = c_raw[a, 0][:, :, h * HALF_S : (h + 1) * HALF_S]
-            interleave(nc.scalar.copy, grouped[:, 0:scalar_cols], rows[:, :, 0:scalar_cols])
-            if scalar_cols < HALF_S:
-                interleave(nc.vector.tensor_copy, grouped[:, scalar_cols:HALF_S], rows[:, :, scalar_cols:HALF_S])
+        def group_c(a, j0, width, copy):
+            grouped = keep.tile([P, width, 4], BF16, name="cg%d_%d" % (a, j0), align_bytes=64)
+            interleave(copy, grouped[:], c_raw[a][:, :, j0 : j0 + width])
             return grouped[:].rearrange("p j i -> p (j i)")
 
         w4_pass = [w4[:, a, :].bitcast(FP4X4) for a in range(PASSES)]
@@ -154,34 +129,22 @@ def tile_list_sage_tm_none_kernel(tc, xT, c, w4_words, w4_scales, w8_words, w8_s
             copy(result, acc[jt][:])
             nc.sync.dma_start(out[jt * P : (jt + 1) * P, :], result)
 
-        def neighbours(a):
-            gather_all(a, 0, cast_pair(a, 0))
-            window = cast_pair(a, 1)
-            gather_half(a, 1, window, 0, 0)
-            gather_half(a, 1, window, 0, 1)
-            gather_half(a, 1, window, 1, 0)
-            low = maximum(a, 0, fresh("low%d" % a))
-            gather_half(a, 1, window, 1, 1)
-            return low
+        for a in range(PASSES):
+            gather_pair(a, 0)
+            gather_pair(a, 1)
+            low = maximum(a, 0, HALF_S)
+            high = maximum(a, HALF_S, HALF_S)
+            xm = quantise(low, "x%dlow" % a) + quantise(high, "x%dhigh" % a)
+            for jt in range(4):
+                multiply(jt, xm[jt], w4_pass[a], s4[:, a, :], a == 0, False)
 
-        low = neighbours(0)
-        multiply(quantise(low, "x00"), 0, w4_pass[0], s4[:, 0, :], True, False)
-        multiply(quantise(maximum(0, 1, fresh("high0")), "x01"), 2, w4_pass[0], s4[:, 0, :], True, False)
-        low = neighbours(1)
-        x10 = quantise(low, "x10")
-        c00 = quantise(group_c(0, 0, HALF_S), "c00")
-        high = maximum(1, 1, fresh("high1"))
-        c01 = quantise(group_c(0, 1, HALF_S), "c01")
-        x11 = quantise(high, "x11")
-        c10 = quantise(group_c(1, 0, HALF_S), "c10")
-        c11 = quantise(group_c(1, 1, 128), "c11")
-        multiply(x10, 0, w4_pass[1], s4[:, 1, :], False, False)
-        multiply(c00, 0, w8_pass[0], s8[:, 0, :], False, False)
-        multiply(c10, 0, w8_pass[1], s8[:, 1, :], False, True)
-        multiply(c01, 2, w8_pass[0], s8[:, 0, :], False, False)
-        multiply(x11, 2, w4_pass[1], s4[:, 1, :], False, False)
-        multiply(c11, 2, w8_pass[1], s8[:, 1, :], False, True)
-        store(0, nc.scalar.copy)
-        store(1, nc.scalar.copy)
-        store(2, nc.vector.tensor_copy)
-        store(3, nc.scalar.copy)
+        first = []
+        for h in range(2):
+            first = first + quantise(group_c(0, h * HALF_S, HALF_S, nc.scalar.copy), "c0%d" % h)
+        second = []
+        for jt in range(4):
+            second = second + quantise(group_c(1, jt * P, P, nc.scalar.copy), "c1%d" % jt)
+        for jt in range(4):
+            multiply(jt, first[jt], w8_pass[0], s8[:, 0, :], False, False)
+            multiply(jt, second[jt], w8_pass[1], s8[:, 1, :], False, True)
+            store(jt, nc.vector.tensor_copy if jt % 2 == 0 else nc.scalar.copy)

@@ -18,9 +18,10 @@ MAX = mybir.AluOpType.max
 P = 128
 PASSES = 2
 HALF_S = S // 2
+RUNS = [(0, 0), (0, 1)]
 CHUNKS = {
-    (0, 0): [(0, 1024, 512), (1024, 2048, 1376)],
-    (0, 1): [(0, 1024, 896), (1024, 2048, 1376)],
+    (0, 0): [(0, 1024, 352), (1024, 2048, 1376)],
+    (0, 1): [(0, 1024, 480), (1024, 2048, 1376)],
     (1, 0): [(0, 1024, 1024), (1024, 2048, 1792)],
     (1, 1): [(0, 1024, 1024), (1024, 1536, 1024), (1536, 2048, 1824)],
 }
@@ -54,9 +55,18 @@ def tile_list_sage_tm_none_kernel(tc, xT, c, w4_words, w4_scales, w8_words, w8_s
         raw = {}
 
         def load_x(a, u):
-            for t0, t1, split in CHUNKS[a, u]:
-                raw[a, u, t0] = keep.tile([P, 2, t1 - t0], F32, name="raw%d%d_%d" % (a, u, t0))
-                nc.sync.dma_start(raw[a, u, t0][:], x_rows[a, :, 2 * u : 2 * u + 2, t0:t1])
+            if (a, u) in RUNS:
+                both = keep.tile([P, 2 * T], F32, name="raw%d%d" % (a, u))
+                source = x_rows[a, :, 2 * u : 2 * u + 2, :].rearrange("p e t -> p (e t)")
+                for t0, t1, split in CHUNKS[a, u]:
+                    begin = T + t0 if t0 > 0 else 0
+                    nc.sync.dma_start(both[:, begin : T + t1], source[:, begin : T + t1])
+                    raw[a, u, t0] = both[:].rearrange("p (e t) -> p e t", e=2)[:, :, t0:t1]
+            else:
+                for t0, t1, split in CHUNKS[a, u]:
+                    chunk = keep.tile([P, 2, t1 - t0], F32, name="raw%d%d_%d" % (a, u, t0))
+                    nc.sync.dma_start(chunk[:], x_rows[a, :, 2 * u : 2 * u + 2, t0:t1])
+                    raw[a, u, t0] = chunk[:]
 
         c_raw = [keep.tile([P, 4, S], F32, name="c%d" % a) for a in range(PASSES)]
 

@@ -18,12 +18,13 @@ MAX = mybir.AluOpType.max
 P = 128
 PASSES = 2
 HALF_S = S // 2
+HALF_M = M // 2
 RUNS = [(0, 0), (0, 1)]
 CHUNKS = {
     (0, 0): [(0, 1024, 352), (1024, 2048, 1376)],
-    (0, 1): [(0, 1024, 480), (1024, 2048, 1376)],
-    (1, 0): [(0, 1024, 1024), (1024, 2048, 1792)],
-    (1, 1): [(0, 1024, 1024), (1024, 1536, 1024), (1536, 2048, 1824)],
+    (0, 1): [(0, 640, 352), (640, 1536, 944), (1536, 2048, 1712)],
+    (1, 0): [(0, 1024, 1024), (1024, 2048, 1712)],
+    (1, 1): [(0, 768, 768), (768, 1536, 1232), (1536, 2048, 1712)],
 }
 
 
@@ -38,16 +39,19 @@ def tile_list_sage_tm_none_kernel(tc, xT, c, w4_words, w4_scales, w8_words, w8_s
         w4 = keep.tile([P, PASSES, 2 * M], U8, name="w4", align_bytes=64)
         w8 = keep.tile([P, PASSES, M], U32, name="w8", align_bytes=64)
         s4 = keep.tile([P, PASSES, M], U8, name="s4", align_bytes=64)
-        s8 = keep.tile([P, PASSES, M], U8, name="s8", align_bytes=64)
+        s8 = keep.tile([P, M], U8, name="s8", align_bytes=64)
         nc.vector.memset(s4[:].bitcast(I32), 0)
         nc.vector.memset(s8[:].bitcast(I32), 0)
 
-        for plane, scales in ((s4, w4_scales), (s8, w8_scales)):
-            for q in range(4):
-                nc.gpsimd.dma_start(
-                    plane[32 * q : 32 * q + 4].bitcast(I32),
-                    scales[:, 4 * q : 4 * q + 4, :].rearrange("a r n -> r a n").bitcast(I32),
-                )
+        for q in range(4):
+            nc.gpsimd.dma_start(
+                s4[32 * q : 32 * q + 4].bitcast(I32),
+                w4_scales[:, 4 * q : 4 * q + 4, :].rearrange("a r n -> r a n").bitcast(I32),
+            )
+        for q in range(4):
+            nc.gpsimd.dma_start(
+                s8[32 * q + 4 : 32 * q + 12].bitcast(I32), w8_scales[:, 4 * q : 4 * q + 4, :].bitcast(I32)
+            )
 
         x_rows = xT.rearrange("(a p i) t -> a p i t", a=PASSES, i=4)
         c_rows = c.rearrange("(a p i) j -> a p i j", a=PASSES, i=4)
@@ -82,7 +86,7 @@ def tile_list_sage_tm_none_kernel(tc, xT, c, w4_words, w4_scales, w8_words, w8_s
         nc.sync.dma_start(w8[:].bitcast(I32), w8_words.rearrange("a p n i -> p a (n i)").bitcast(I32))
 
         picked = [keep.tile([P, 2, G, S], U32, name="picked%d" % a) for a in range(PASSES)]
-        acc = [psum.tile([P, M], F32, name="acc%d" % jt) for jt in range(4)]
+        acc = [[psum.tile([P, HALF_M], F32, name="acc%d%d" % (jt, h)) for h in range(2)] for jt in range(4)]
 
         def interleave(copy, grouped, rows):
             copy(grouped.rearrange("p (b t) e -> p b e t", t=4), rows.rearrange("p e (b t) -> p b e t", t=4))
@@ -114,30 +118,32 @@ def tile_list_sage_tm_none_kernel(tc, xT, c, w4_words, w4_scales, w8_words, w8_s
             nc.vector.quantize_mx(out=codes[:].bitcast(FP8X4), scales=scales[:], in_=grouped)
             return [(codes[:, b * P : (b + 1) * P], scales[:, b * P : (b + 1) * P]) for b in range(width // P)]
 
-        def multiply(jt, operand, weights, plane, start, stop):
+        def multiply(jt, operand, weights, plane, width, start, stop):
             codes, scales = operand
-            nc.tensor.matmul_mx(
-                out=acc[jt][:],
-                lhsT=codes.bitcast(FP8X4),
-                lhsT_scale=scales,
-                rhs=weights,
-                rhs_scale=plane,
-                start=start,
-                stop=stop,
-            )
+            per_column = weights.shape[1] // M
+            kind = FP4X4 if per_column == 2 else FP8X4
+            for n0 in range(0, M, width):
+                at = n0 % HALF_M
+                nc.tensor.matmul_mx(
+                    out=acc[jt][n0 // HALF_M][:, at : at + width],
+                    lhsT=codes.bitcast(FP8X4),
+                    lhsT_scale=scales,
+                    rhs=weights[:, per_column * n0 : per_column * (n0 + width)].bitcast(kind),
+                    rhs_scale=plane[:, n0 : n0 + width],
+                    start=start and at == 0,
+                    stop=stop and at + width == HALF_M,
+                )
 
         def group_c(a, j0, width, copy):
             grouped = keep.tile([P, width, 4], BF16, name="cg%d_%d" % (a, j0), align_bytes=64)
             interleave(copy, grouped[:], c_raw[a][:, :, j0 : j0 + width])
             return grouped[:].rearrange("p j i -> p (j i)")
 
-        w4_pass = [w4[:, a, :].bitcast(FP4X4) for a in range(PASSES)]
-        w8_pass = [w8[:, a, :].bitcast(FP8X4) for a in range(PASSES)]
-
-        def store(jt, copy):
-            result = keep.tile([P, M], F32, name="result%d" % jt)[:]
-            copy(result, acc[jt][:])
-            nc.sync.dma_start(out[jt * P : (jt + 1) * P, :], result)
+        def store(jt):
+            result = keep.tile([P, M], F32, name="result%d" % jt)
+            nc.scalar.copy(result[:, 0:HALF_M], acc[jt][0][:])
+            nc.vector.tensor_copy(result[:, HALF_M:M], acc[jt][1][:])
+            nc.sync.dma_start(out[jt * P : (jt + 1) * P, :], result[:])
 
         for a in range(PASSES):
             gather_pair(a, 0)
@@ -146,7 +152,7 @@ def tile_list_sage_tm_none_kernel(tc, xT, c, w4_words, w4_scales, w8_words, w8_s
             high = maximum(a, HALF_S, HALF_S)
             xm = quantise(low, "x%dlow" % a) + quantise(high, "x%dhigh" % a)
             for jt in range(4):
-                multiply(jt, xm[jt], w4_pass[a], s4[:, a, :], a == 0, False)
+                multiply(jt, xm[jt], w4[:, a, :], s4[:, a, :], P, a == 0, False)
 
         first = []
         for h in range(2):
@@ -155,6 +161,6 @@ def tile_list_sage_tm_none_kernel(tc, xT, c, w4_words, w4_scales, w8_words, w8_s
         for jt in range(4):
             second = second + quantise(group_c(1, jt * P, P, nc.scalar.copy), "c1%d" % jt)
         for jt in range(4):
-            multiply(jt, first[jt], w8_pass[0], s8[:, 0, :], False, False)
-            multiply(jt, second[jt], w8_pass[1], s8[:, 1, :], False, True)
-            store(jt, nc.vector.tensor_copy if jt % 2 == 0 else nc.scalar.copy)
+            multiply(jt, first[jt], w8[:, 0, :], s8[4:P, :], HALF_M, False, False)
+            multiply(jt, second[jt], w8[:, 1, :], s8[8:P, :], HALF_M, False, True)
+            store(jt)

@@ -13,18 +13,19 @@ U16 = mybir.dt.uint16
 U8 = mybir.dt.uint8
 FP8X4 = mybir.dt.float8_e4m3fn_x4
 FP4X4 = mybir.dt.float4_e2m1fn_x4
-MAX = mybir.AluOpType.max
 
 P = 128
-PASSES = 2
+PASSES = K // (4 * P)
+NODE_TILES = S // P
 HALF_S = S // 2
 HALF_M = M // 2
-RUNS = [(0, 0), (0, 1)]
+RUN = 4
+
 CHUNKS = {
-    (0, 0): [(0, 1024, 352), (1024, 2048, 1376)],
-    (0, 1): [(0, 640, 352), (640, 1536, 944), (1536, 2048, 1712)],
-    (1, 0): [(0, 1024, 1024), (1024, 2048, 1712)],
-    (1, 1): [(0, 768, 768), (768, 1536, 1232), (1536, 2048, 1712)],
+    (0, 0): [(0, T // 2, 1), (T // 2, T, 1)],
+    (0, 1): [(0, 3 * T // 8, 1), (3 * T // 8, 3 * T // 4, 1), (3 * T // 4, T, 1)],
+    (1, 0): [(0, T // 2, 3), (T // 2, T, 2)],
+    (1, 1): [(0, 3 * T // 8, 3), (3 * T // 8, 3 * T // 4, 2), (3 * T // 4, T, 1)],
 }
 
 
@@ -37,7 +38,8 @@ def tile_list_sage_tm_none_kernel(tc, xT, c, w4_words, w4_scales, w8_words, w8_s
         offsets = keep.tile([P, G * S // 16], U16, name="offsets")
 
         w4 = keep.tile([P, PASSES, 2 * M], U8, name="w4", align_bytes=64)
-        w8 = keep.tile([P, PASSES, M], U32, name="w8", align_bytes=64)
+        w8 = [keep.tile([P, PASSES, HALF_M], U32, name="w8_%d" % h, align_bytes=64) for h in range(2)]
+
         s4 = keep.tile([P, PASSES, M], U8, name="s4", align_bytes=64)
         s8 = keep.tile([P, M], U8, name="s8", align_bytes=64)
         nc.vector.memset(s4[:].bitcast(I32), 0)
@@ -55,61 +57,70 @@ def tile_list_sage_tm_none_kernel(tc, xT, c, w4_words, w4_scales, w8_words, w8_s
 
         x_rows = xT.rearrange("(a p i) t -> a p i t", a=PASSES, i=4)
         c_rows = c.rearrange("(a p i) j -> a p i j", a=PASSES, i=4)
+        w8_rows = w8_words.rearrange("a p n i -> p a (n i)").bitcast(I32)
+        x_raw = {}
 
-        raw = {}
+        def load_pair_in_runs(a, u):
+            both = keep.tile([P, 2 * T], F32, name="x%d%d" % (a, u))
+            source = x_rows[a, :, 2 * u : 2 * u + 2, :].rearrange("p e t -> p (e t)")
+            for t0, t1, thirds in CHUNKS[a, u]:
+                begin = T + t0 if t0 > 0 else 0
+                nc.sync.dma_start(both[:, begin : T + t1], source[:, begin : T + t1])
+                x_raw[a, u, t0] = both[:].rearrange("p (e t) -> p e t", e=2)[:, :, t0:t1]
 
-        def load_x(a, u):
-            if (a, u) in RUNS:
-                both = keep.tile([P, 2 * T], F32, name="raw%d%d" % (a, u))
-                source = x_rows[a, :, 2 * u : 2 * u + 2, :].rearrange("p e t -> p (e t)")
-                for t0, t1, split in CHUNKS[a, u]:
-                    begin = T + t0 if t0 > 0 else 0
-                    nc.sync.dma_start(both[:, begin : T + t1], source[:, begin : T + t1])
-                    raw[a, u, t0] = both[:].rearrange("p (e t) -> p e t", e=2)[:, :, t0:t1]
-            else:
-                for t0, t1, split in CHUNKS[a, u]:
-                    chunk = keep.tile([P, 2, t1 - t0], F32, name="raw%d%d_%d" % (a, u, t0))
-                    nc.sync.dma_start(chunk[:], x_rows[a, :, 2 * u : 2 * u + 2, t0:t1])
-                    raw[a, u, t0] = chunk[:]
+        def load_pair_in_columns(a, u):
+            for t0, t1, thirds in CHUNKS[a, u]:
+                chunk = keep.tile([P, 2, t1 - t0], F32, name="x%d%d_%d" % (a, u, t0))
+                nc.sync.dma_start(chunk[:], x_rows[a, :, 2 * u : 2 * u + 2, t0:t1])
+                x_raw[a, u, t0] = chunk[:]
 
         c_raw = [keep.tile([P, 4, S], F32, name="c%d" % a) for a in range(PASSES)]
 
-        load_x(0, 0)
+        load_pair_in_runs(0, 0)
         nc.sync.dma_start(offsets[:], offs)
-        load_x(0, 1)
-        load_x(1, 0)
-        load_x(1, 1)
-        nc.sync.dma_start(c_raw[0][:], c_rows[0])
-        nc.sync.dma_start(w4[:, 0].bitcast(I32), w4_words[0].bitcast(I32))
-        nc.sync.dma_start(c_raw[1][:], c_rows[1])
-        nc.sync.dma_start(w4[:, 1].bitcast(I32), w4_words[1].bitcast(I32))
-        nc.sync.dma_start(w8[:].bitcast(I32), w8_words.rearrange("a p n i -> p a (n i)").bitcast(I32))
+        load_pair_in_runs(0, 1)
+        load_pair_in_columns(1, 0)
+        load_pair_in_columns(1, 1)
+        for a in range(PASSES):
+            nc.sync.dma_start(c_raw[a][:], c_rows[a])
+            nc.sync.dma_start(w4[:, a].bitcast(I32), w4_words[a].bitcast(I32))
+        for h in range(2):
+            nc.sync.dma_start(w8[h][:].bitcast(I32), w8_rows[:, :, h * HALF_M : (h + 1) * HALF_M])
 
         picked = [keep.tile([P, 2, G, S], U32, name="picked%d" % a) for a in range(PASSES)]
-        acc = [[psum.tile([P, HALF_M], F32, name="acc%d%d" % (jt, h)) for h in range(2)] for jt in range(4)]
+        acc = [[psum.tile([P, HALF_M], F32, name="acc%d%d" % (jt, h)) for h in range(2)] for jt in range(NODE_TILES)]
 
         def interleave(copy, grouped, rows):
-            copy(grouped.rearrange("p (b t) e -> p b e t", t=4), rows.rearrange("p e (b t) -> p b e t", t=4))
+            copy(grouped.rearrange("p (b t) e -> p b e t", t=RUN), rows.rearrange("p e (b t) -> p b e t", t=RUN))
 
         def gather_pair(a, u):
             table = keep.tile([P, T, 2], BF16, name="table%d%d" % (a, u))
-            for t0, t1, split in CHUNKS[a, u]:
-                rows = raw[a, u, t0]
-                if split > t0:
-                    interleave(nc.scalar.copy, table[:, t0:split], rows[:, :, 0 : split - t0])
+            for t0, t1, thirds in CHUNKS[a, u]:
+                rows = x_raw[a, u, t0]
+                scalar_columns = (t1 - t0) * thirds // 3 // (2 * RUN) * (2 * RUN)
+                split = t0 + scalar_columns
+                interleave(nc.scalar.copy, table[:, t0:split], rows[:, :, 0:scalar_columns])
                 if split < t1:
-                    interleave(nc.vector.tensor_copy, table[:, split:t1], rows[:, :, split - t0 : t1 - t0])
+                    interleave(nc.vector.tensor_copy, table[:, split:t1], rows[:, :, scalar_columns : t1 - t0])
             window = table[:].rearrange("p t e -> p (t e)").bitcast(U32)
             nc.vector.tensor_copy(picked[a][:, u].rearrange("p g j -> p (g j)"), window.indirect(offsets[:]))
 
-        def maximum(a, j0, width):
-            grouped = keep.tile([P, 4 * width], BF16, name="xm%d_%d" % (a, j0), align_bytes=64)
-            pairs = picked[a][:].bitcast(BF16).rearrange("p u g (j e) -> p g j u e", e=2)
-            cols = slice(j0, j0 + width)
+        def maximum(a, j0):
+            grouped = keep.tile([P, 4 * HALF_S], BF16, name="xm%d_%d" % (a, j0), align_bytes=64)
+            values = picked[a][:].bitcast(BF16).rearrange("p u g (j e) -> p g j u e", e=2)
+            nodes = slice(j0, j0 + HALF_S)
             nc.vector.tensor_tensor(
-                grouped[:].rearrange("p (j u e) -> p j u e", u=2, e=2), pairs[:, 0, cols], pairs[:, 1, cols], MAX
+                grouped[:].rearrange("p (j u e) -> p j u e", u=2, e=2),
+                values[:, 0, nodes],
+                values[:, 1, nodes],
+                mybir.AluOpType.max,
             )
             return grouped[:]
+
+        def group_c(a, j0, width):
+            grouped = keep.tile([P, width, 4], BF16, name="cg%d_%d" % (a, j0), align_bytes=64)
+            interleave(nc.scalar.copy, grouped[:], c_raw[a][:, :, j0 : j0 + width])
+            return grouped[:].rearrange("p j i -> p (j i)")
 
         def quantise(grouped, name):
             width = grouped.shape[1] // 4
@@ -118,49 +129,55 @@ def tile_list_sage_tm_none_kernel(tc, xT, c, w4_words, w4_scales, w8_words, w8_s
             nc.vector.quantize_mx(out=codes[:].bitcast(FP8X4), scales=scales[:], in_=grouped)
             return [(codes[:, b * P : (b + 1) * P], scales[:, b * P : (b + 1) * P]) for b in range(width // P)]
 
-        def multiply(jt, operand, weights, plane, width, start, stop):
+        def multiply_neighbours(jt, a, operand):
             codes, scales = operand
-            per_column = weights.shape[1] // M
-            kind = FP4X4 if per_column == 2 else FP8X4
-            for n0 in range(0, M, width):
+            for n0 in range(0, M, P):
                 at = n0 % HALF_M
                 nc.tensor.matmul_mx(
-                    out=acc[jt][n0 // HALF_M][:, at : at + width],
+                    out=acc[jt][n0 // HALF_M][:, at : at + P],
                     lhsT=codes.bitcast(FP8X4),
                     lhsT_scale=scales,
-                    rhs=weights[:, per_column * n0 : per_column * (n0 + width)].bitcast(kind),
-                    rhs_scale=plane[:, n0 : n0 + width],
-                    start=start and at == 0,
-                    stop=stop and at + width == HALF_M,
+                    rhs=w4[:, a, 2 * n0 : 2 * (n0 + P)].bitcast(FP4X4),
+                    rhs_scale=s4[:, a, n0 : n0 + P],
+                    start=a == 0 and at == 0,
+                    stop=False,
                 )
 
-        def group_c(a, j0, width, copy):
-            grouped = keep.tile([P, width, 4], BF16, name="cg%d_%d" % (a, j0), align_bytes=64)
-            interleave(copy, grouped[:], c_raw[a][:, :, j0 : j0 + width])
-            return grouped[:].rearrange("p j i -> p (j i)")
+        def multiply_own(jt, h, a, operand):
+            codes, scales = operand
+            nc.tensor.matmul_mx(
+                out=acc[jt][h][:],
+                lhsT=codes.bitcast(FP8X4),
+                lhsT_scale=scales,
+                rhs=w8[h][:, a, :].bitcast(FP8X4),
+                rhs_scale=s8[4 + 4 * a : P, h * HALF_M : (h + 1) * HALF_M],
+                start=False,
+                stop=a == PASSES - 1,
+            )
 
-        def store(jt):
-            result = keep.tile([P, M], F32, name="result%d" % jt)
-            nc.scalar.copy(result[:, 0:HALF_M], acc[jt][0][:])
-            nc.vector.tensor_copy(result[:, HALF_M:M], acc[jt][1][:])
-            nc.sync.dma_start(out[jt * P : (jt + 1) * P, :], result[:])
+        def store(jt, h, copy):
+            result = keep.tile([P, HALF_M], F32, name="result%d%d" % (jt, h))
+            copy(result[:], acc[jt][h][:])
+            nc.sync.dma_start(out[jt * P : (jt + 1) * P, h * HALF_M : (h + 1) * HALF_M], result[:])
 
         for a in range(PASSES):
             gather_pair(a, 0)
             gather_pair(a, 1)
-            low = maximum(a, 0, HALF_S)
-            high = maximum(a, HALF_S, HALF_S)
+            low = maximum(a, 0)
+            high = maximum(a, HALF_S)
             xm = quantise(low, "x%dlow" % a) + quantise(high, "x%dhigh" % a)
-            for jt in range(4):
-                multiply(jt, xm[jt], w4[:, a, :], s4[:, a, :], P, a == 0, False)
+            for jt in range(NODE_TILES):
+                multiply_neighbours(jt, a, xm[jt])
 
-        first = []
-        for h in range(2):
-            first = first + quantise(group_c(0, h * HALF_S, HALF_S, nc.scalar.copy), "c0%d" % h)
-        second = []
-        for jt in range(4):
-            second = second + quantise(group_c(1, jt * P, P, nc.scalar.copy), "c1%d" % jt)
-        for jt in range(4):
-            multiply(jt, first[jt], w8[:, 0, :], s8[4:P, :], HALF_M, False, False)
-            multiply(jt, second[jt], w8[:, 1, :], s8[8:P, :], HALF_M, False, True)
-            store(jt)
+        c_first = []
+        for j0 in range(0, S, HALF_S):
+            c_first = c_first + quantise(group_c(0, j0, HALF_S), "c0_%d" % j0)
+        c_second = []
+        for j0 in range(0, S, P):
+            c_second = c_second + quantise(group_c(1, j0, P), "c1_%d" % j0)
+
+        for jt in range(NODE_TILES):
+            for h, copy in enumerate((nc.vector.tensor_copy, nc.scalar.copy)):
+                multiply_own(jt, h, 0, c_first[jt])
+                multiply_own(jt, h, 1, c_second[jt])
+                store(jt, h, copy)

@@ -22,10 +22,10 @@ HALF_M = M // 2
 RUN = 4
 
 CHUNKS = {
-    (0, 0): [(0, T // 2, 1), (T // 2, T, 1)],
-    (0, 1): [(0, 3 * T // 8, 1), (3 * T // 8, 3 * T // 4, 1), (3 * T // 4, T, 1)],
-    (1, 0): [(0, T // 2, 3), (T // 2, T, 2)],
-    (1, 1): [(0, 3 * T // 8, 3), (3 * T // 8, 3 * T // 4, 2), (3 * T // 4, T, 1)],
+    (0, 0): [(0, T // 2, 2), (T // 2, T, 2)],
+    (0, 1): [(0, 3 * T // 8, 2), (3 * T // 8, 3 * T // 4, 2), (3 * T // 4, T, 2)],
+    (1, 0): [(0, 3 * T // 8, 6), (3 * T // 8, T, 3)],
+    (1, 1): [(0, T // 4, 6), (T // 4, 3 * T // 4, 3), (3 * T // 4, T, 2)],
 }
 
 
@@ -38,7 +38,7 @@ def tile_list_sage_tm_none_kernel(tc, xT, c, w4_words, w4_scales, w8_words, w8_s
         offsets = keep.tile([P, G * S // 16], U16, name="offsets")
 
         w4 = keep.tile([P, PASSES, 2 * M], U8, name="w4", align_bytes=64)
-        w8 = [keep.tile([P, PASSES, HALF_M], U32, name="w8_%d" % h, align_bytes=64) for h in range(2)]
+        w8 = keep.tile([P, PASSES, M], U32, name="w8", align_bytes=64)
 
         s4 = keep.tile([P, PASSES, M], U8, name="s4", align_bytes=64)
         s8 = keep.tile([P, M], U8, name="s8", align_bytes=64)
@@ -57,35 +57,27 @@ def tile_list_sage_tm_none_kernel(tc, xT, c, w4_words, w4_scales, w8_words, w8_s
 
         x_rows = xT.rearrange("(a p i) t -> a p i t", a=PASSES, i=4)
         c_rows = c.rearrange("(a p i) j -> a p i j", a=PASSES, i=4)
-        w8_rows = w8_words.rearrange("a p n i -> p a (n i)").bitcast(I32)
         x_raw = {}
 
-        def load_pair_in_runs(a, u):
+        def load_pair(a, u):
             both = keep.tile([P, 2 * T], F32, name="x%d%d" % (a, u))
             source = x_rows[a, :, 2 * u : 2 * u + 2, :].rearrange("p e t -> p (e t)")
-            for t0, t1, thirds in CHUNKS[a, u]:
+            for t0, t1, sixths in CHUNKS[a, u]:
                 begin = T + t0 if t0 > 0 else 0
                 nc.sync.dma_start(both[:, begin : T + t1], source[:, begin : T + t1])
                 x_raw[a, u, t0] = both[:].rearrange("p (e t) -> p e t", e=2)[:, :, t0:t1]
 
-        def load_pair_in_columns(a, u):
-            for t0, t1, thirds in CHUNKS[a, u]:
-                chunk = keep.tile([P, 2, t1 - t0], F32, name="x%d%d_%d" % (a, u, t0))
-                nc.sync.dma_start(chunk[:], x_rows[a, :, 2 * u : 2 * u + 2, t0:t1])
-                x_raw[a, u, t0] = chunk[:]
-
         c_raw = [keep.tile([P, 4, S], F32, name="c%d" % a) for a in range(PASSES)]
 
-        load_pair_in_runs(0, 0)
+        load_pair(0, 0)
         nc.sync.dma_start(offsets[:], offs)
-        load_pair_in_runs(0, 1)
-        load_pair_in_columns(1, 0)
-        load_pair_in_columns(1, 1)
+        load_pair(0, 1)
+        load_pair(1, 0)
+        load_pair(1, 1)
         for a in range(PASSES):
             nc.sync.dma_start(c_raw[a][:], c_rows[a])
             nc.sync.dma_start(w4[:, a].bitcast(I32), w4_words[a].bitcast(I32))
-        for h in range(2):
-            nc.sync.dma_start(w8[h][:].bitcast(I32), w8_rows[:, :, h * HALF_M : (h + 1) * HALF_M])
+        nc.sync.dma_start(w8[:].bitcast(I32), w8_words.rearrange("a p n i -> p a (n i)").bitcast(I32))
 
         picked = [keep.tile([P, 2, G, S], U32, name="picked%d" % a) for a in range(PASSES)]
         acc = [[psum.tile([P, HALF_M], F32, name="acc%d%d" % (jt, h)) for h in range(2)] for jt in range(NODE_TILES)]
@@ -95,9 +87,9 @@ def tile_list_sage_tm_none_kernel(tc, xT, c, w4_words, w4_scales, w8_words, w8_s
 
         def gather_pair(a, u):
             table = keep.tile([P, T, 2], BF16, name="table%d%d" % (a, u))
-            for t0, t1, thirds in CHUNKS[a, u]:
+            for t0, t1, sixths in CHUNKS[a, u]:
                 rows = x_raw[a, u, t0]
-                scalar_columns = (t1 - t0) * thirds // 3 // (2 * RUN) * (2 * RUN)
+                scalar_columns = (t1 - t0) * sixths // 6 // (2 * RUN) * (2 * RUN)
                 split = t0 + scalar_columns
                 interleave(nc.scalar.copy, table[:, t0:split], rows[:, :, 0:scalar_columns])
                 if split < t1:
@@ -143,22 +135,25 @@ def tile_list_sage_tm_none_kernel(tc, xT, c, w4_words, w4_scales, w8_words, w8_s
                     stop=False,
                 )
 
-        def multiply_own(jt, h, a, operand):
+        def multiply_own(jt, a, operand):
             codes, scales = operand
-            nc.tensor.matmul_mx(
-                out=acc[jt][h][:],
-                lhsT=codes.bitcast(FP8X4),
-                lhsT_scale=scales,
-                rhs=w8[h][:, a, :].bitcast(FP8X4),
-                rhs_scale=s8[4 + 4 * a : P, h * HALF_M : (h + 1) * HALF_M],
-                start=False,
-                stop=a == PASSES - 1,
-            )
+            for h in range(2):
+                columns = slice(h * HALF_M, (h + 1) * HALF_M)
+                nc.tensor.matmul_mx(
+                    out=acc[jt][h][:],
+                    lhsT=codes.bitcast(FP8X4),
+                    lhsT_scale=scales,
+                    rhs=w8[:, a, columns].bitcast(FP8X4),
+                    rhs_scale=s8[4 + 4 * a : P, columns],
+                    start=False,
+                    stop=a == PASSES - 1,
+                )
 
-        def store(jt, h, copy):
-            result = keep.tile([P, HALF_M], F32, name="result%d%d" % (jt, h))
-            copy(result[:], acc[jt][h][:])
-            nc.sync.dma_start(out[jt * P : (jt + 1) * P, h * HALF_M : (h + 1) * HALF_M], result[:])
+        def store(jt):
+            result = keep.tile([P, M], F32, name="result%d" % jt)
+            nc.scalar.copy(result[:, 0:HALF_M], acc[jt][0][:])
+            nc.vector.tensor_copy(result[:, HALF_M:M], acc[jt][1][:])
+            nc.sync.dma_start(out[jt * P : (jt + 1) * P, :], result[:])
 
         for a in range(PASSES):
             gather_pair(a, 0)
@@ -177,7 +172,6 @@ def tile_list_sage_tm_none_kernel(tc, xT, c, w4_words, w4_scales, w8_words, w8_s
             c_second = c_second + quantise(group_c(1, j0, P), "c1_%d" % j0)
 
         for jt in range(NODE_TILES):
-            for h, copy in enumerate((nc.vector.tensor_copy, nc.scalar.copy)):
-                multiply_own(jt, h, 0, c_first[jt])
-                multiply_own(jt, h, 1, c_second[jt])
-                store(jt, h, copy)
+            multiply_own(jt, 0, c_first[jt])
+            multiply_own(jt, 1, c_second[jt])
+            store(jt)

@@ -25,7 +25,7 @@ CHUNKS = {
     (0, 0): [(0, T // 2, 2), (T // 2, T, 2)],
     (0, 1): [(0, 3 * T // 8, 2), (3 * T // 8, 3 * T // 4, 2), (3 * T // 4, T, 2)],
     (1, 0): [(0, 3 * T // 8, 6), (3 * T // 8, T, 3)],
-    (1, 1): [(0, T // 4, 6), (T // 4, 3 * T // 4, 3), (3 * T // 4, T, 2)],
+    (1, 1): [(0, 7 * T // 16, 6), (7 * T // 16, 3 * T // 4, 3), (3 * T // 4, T, 2)],
 }
 
 
@@ -67,16 +67,30 @@ def tile_list_sage_tm_none_kernel(tc, xT, c, w4_words, w4_scales, w8_words, w8_s
                 nc.sync.dma_start(both[:, begin : T + t1], source[:, begin : T + t1])
                 x_raw[a, u, t0] = both[:].rearrange("p (e t) -> p e t", e=2)[:, :, t0:t1]
 
+        def load_last_pair(a, u):
+            lead_end = CHUNKS[a, u][0][1]
+            lead = keep.tile([P, 2, lead_end], F32, name="x_lead")
+            rest = keep.tile([P, 2, T - lead_end], F32, name="x_rest")
+            nc.sync.dma_start(lead[:], x_rows[a, :, 2 * u : 2 * u + 2, 0:lead_end])
+            x_raw[a, u, 0] = lead[:]
+            nc.sync.dma_start(rest[:, 0], x_rows[a, :, 2 * u, lead_end:T])
+            for t0, t1, sixths in CHUNKS[a, u][1:]:
+                columns = slice(t0 - lead_end, t1 - lead_end)
+                nc.sync.dma_start(rest[:, 1, columns], x_rows[a, :, 2 * u + 1, t0:t1])
+                x_raw[a, u, t0] = rest[:, :, columns]
+
         c_raw = [keep.tile([P, 4, S], F32, name="c%d" % a) for a in range(PASSES)]
 
         load_pair(0, 0)
         nc.sync.dma_start(offsets[:], offs)
         load_pair(0, 1)
         load_pair(1, 0)
-        load_pair(1, 1)
-        for a in range(PASSES):
-            nc.sync.dma_start(c_raw[a][:], c_rows[a])
-            nc.sync.dma_start(w4[:, a].bitcast(I32), w4_words[a].bitcast(I32))
+        load_last_pair(1, 1)
+        nc.sync.dma_start(c_raw[0][:, 0:3], c_rows[0, :, 0:3])
+        nc.sync.dma_start(w4[:, 0].bitcast(I32), w4_words[0].bitcast(I32))
+        nc.sync.dma_start(c_raw[0][:, 3], c_rows[0, :, 3])
+        nc.sync.dma_start(c_raw[1][:], c_rows[1])
+        nc.sync.dma_start(w4[:, 1].bitcast(I32), w4_words[1].bitcast(I32))
         nc.sync.dma_start(w8[:].bitcast(I32), w8_words.rearrange("a p n i -> p a (n i)").bitcast(I32))
 
         picked = [keep.tile([P, 2, G, S], U32, name="picked%d" % a) for a in range(PASSES)]
@@ -109,9 +123,9 @@ def tile_list_sage_tm_none_kernel(tc, xT, c, w4_words, w4_scales, w8_words, w8_s
             )
             return grouped[:]
 
-        def group_c(a, j0, width):
+        def group_c(a, j0, width, copy):
             grouped = keep.tile([P, width, 4], BF16, name="cg%d_%d" % (a, j0), align_bytes=64)
-            interleave(nc.scalar.copy, grouped[:], c_raw[a][:, :, j0 : j0 + width])
+            interleave(copy, grouped[:], c_raw[a][:, :, j0 : j0 + width])
             return grouped[:].rearrange("p j i -> p (j i)")
 
         def quantise(grouped, name):
@@ -164,12 +178,11 @@ def tile_list_sage_tm_none_kernel(tc, xT, c, w4_words, w4_scales, w8_words, w8_s
             for jt in range(NODE_TILES):
                 multiply_neighbours(jt, a, xm[jt])
 
-        c_first = []
-        for j0 in range(0, S, HALF_S):
-            c_first = c_first + quantise(group_c(0, j0, HALF_S), "c0_%d" % j0)
+        c_first = quantise(group_c(0, 0, S, nc.scalar.copy), "c0")
         c_second = []
-        for j0 in range(0, S, P):
-            c_second = c_second + quantise(group_c(1, j0, P), "c1_%d" % j0)
+        for jt in range(NODE_TILES):
+            copy = nc.vector.tensor_copy if jt == NODE_TILES - 1 else nc.scalar.copy
+            c_second = c_second + quantise(group_c(1, jt * P, P, copy), "c1_%d" % jt)
 
         for jt in range(NODE_TILES):
             multiply_own(jt, 0, c_first[jt])

@@ -23,7 +23,7 @@ RUN = 4
 
 CHUNKS = {
     (0, 0): [(0, T // 2, 2), (T // 2, T, 2)],
-    (0, 1): [(0, 3 * T // 8, 2), (3 * T // 8, 3 * T // 4, 2), (3 * T // 4, T, 2)],
+    (0, 1): [(0, T // 2, 3), (T // 2, T, 2)],
     (1, 0): [(0, 3 * T // 8, 6), (3 * T // 8, T, 3)],
     (1, 1): [(0, 7 * T // 16, 6), (7 * T // 16, 3 * T // 4, 3), (3 * T // 4, T, 2)],
 }
@@ -79,7 +79,9 @@ def tile_list_sage_tm_none_kernel(tc, xT, c, w4_words, w4_scales, w8_words, w8_s
                 nc.sync.dma_start(rest[:, 1, columns], x_rows[a, :, 2 * u + 1, t0:t1])
                 x_raw[a, u, t0] = rest[:, :, columns]
 
-        c_raw = [keep.tile([P, 4, S], F32, name="c%d" % a) for a in range(PASSES)]
+        c_first_raw = keep.tile([P, 4, S], F32, name="c_first_raw")
+        margin_and_c = keep.tile([P, P + 4 * S], F32, name="margin_and_c", align_bytes=64)
+        c_raw = [c_first_raw[:], margin_and_c[:, P : P + 4 * S].rearrange("p (i j) -> p i j", i=4)]
 
         load_pair(0, 0)
         nc.sync.dma_start(offsets[:], offs)
@@ -89,9 +91,10 @@ def tile_list_sage_tm_none_kernel(tc, xT, c, w4_words, w4_scales, w8_words, w8_s
         nc.sync.dma_start(c_raw[0][:, 0:3], c_rows[0, :, 0:3])
         nc.sync.dma_start(w4[:, 0].bitcast(I32), w4_words[0].bitcast(I32))
         nc.sync.dma_start(c_raw[0][:, 3], c_rows[0, :, 3])
-        nc.sync.dma_start(c_raw[1][:], c_rows[1])
         nc.sync.dma_start(w4[:, 1].bitcast(I32), w4_words[1].bitcast(I32))
-        nc.sync.dma_start(w8[:].bitcast(I32), w8_words.rearrange("a p n i -> p a (n i)").bitcast(I32))
+        nc.sync.dma_start(margin_and_c[:, P : P + 4 * S], c_rows[1].rearrange("p i j -> p (i j)"))
+        for a in range(PASSES):
+            nc.sync.dma_start(w8[:, a].bitcast(I32), w8_words[a].rearrange("p n i -> p (n i)").bitcast(I32))
 
         picked = [keep.tile([P, 2, G, S], U32, name="picked%d" % a) for a in range(PASSES)]
         acc = [[psum.tile([P, HALF_M], F32, name="acc%d%d" % (jt, h)) for h in range(2)] for jt in range(NODE_TILES)]
@@ -109,28 +112,33 @@ def tile_list_sage_tm_none_kernel(tc, xT, c, w4_words, w4_scales, w8_words, w8_s
                 if split < t1:
                     interleave(nc.vector.tensor_copy, table[:, split:t1], rows[:, :, scalar_columns : t1 - t0])
             window = table[:].rearrange("p t e -> p (t e)").bitcast(U32)
-            nc.vector.tensor_copy(picked[a][:, u].rearrange("p g j -> p (g j)"), window.indirect(offsets[:]))
+            words = picked[a][:, u].rearrange("p g j -> p (g j)")
+            cuts = [0, G * S - HALF_S, G * S] if u == 1 else [0, G * S]
+            for m0, m1 in zip(cuts, cuts[1:]):
+                nc.vector.tensor_copy(words[:, m0:m1], window.indirect(offsets[:, m0 // 16 : m1 // 16]))
 
-        def maximum(a, j0):
-            grouped = keep.tile([P, 4 * HALF_S], BF16, name="xm%d_%d" % (a, j0), align_bytes=64)
+        def grouped_tile(name, nodes):
+            return keep.tile([P, 4 * nodes], BF16, name=name, align_bytes=64)[:]
+
+        def maximum(a, j0, grouped):
             values = picked[a][:].bitcast(BF16).rearrange("p u g (j e) -> p g j u e", e=2)
-            nodes = slice(j0, j0 + HALF_S)
+            nodes = slice(j0, j0 + grouped.shape[1] // 4)
             nc.vector.tensor_tensor(
-                grouped[:].rearrange("p (j u e) -> p j u e", u=2, e=2),
+                grouped.rearrange("p (j u e) -> p j u e", u=2, e=2),
                 values[:, 0, nodes],
                 values[:, 1, nodes],
                 mybir.AluOpType.max,
             )
-            return grouped[:]
+            return grouped
 
-        def group_c(a, j0, width, copy):
-            grouped = keep.tile([P, width, 4], BF16, name="cg%d_%d" % (a, j0), align_bytes=64)
-            interleave(copy, grouped[:], c_raw[a][:, :, j0 : j0 + width])
-            return grouped[:].rearrange("p j i -> p (j i)")
-
-        def quantise(grouped, name):
+        def group_c(a, j0, grouped, copy):
             width = grouped.shape[1] // 4
-            codes = keep.tile([P, width], U32, name="codes_" + name, align_bytes=64)
+            interleave(copy, grouped.rearrange("p (j i) -> p j i", i=4), c_raw[a][:, :, j0 : j0 + width])
+            return grouped
+
+        def quantise(grouped, name, tag=""):
+            width = grouped.shape[1] // 4
+            codes = keep.tile([P, width], U32, name="codes_" + name, tag=tag, align_bytes=64)
             scales = keep.tile([P, width], U8, name="scales_" + name, align_bytes=64)
             nc.vector.quantize_mx(out=codes[:].bitcast(FP8X4), scales=scales[:], in_=grouped)
             return [(codes[:, b * P : (b + 1) * P], scales[:, b * P : (b + 1) * P]) for b in range(width // P)]
@@ -169,22 +177,43 @@ def tile_list_sage_tm_none_kernel(tc, xT, c, w4_words, w4_scales, w8_words, w8_s
             nc.vector.tensor_copy(result[:, HALF_M:M], acc[jt][1][:])
             nc.sync.dma_start(out[jt * P : (jt + 1) * P, :], result[:])
 
-        for a in range(PASSES):
-            gather_pair(a, 0)
-            gather_pair(a, 1)
-            low = maximum(a, 0)
-            high = maximum(a, HALF_S)
-            xm = quantise(low, "x%dlow" % a) + quantise(high, "x%dhigh" % a)
-            for jt in range(NODE_TILES):
-                multiply_neighbours(jt, a, xm[jt])
-
-        c_first = quantise(group_c(0, 0, S, nc.scalar.copy), "c0")
-        c_second = []
+        gather_pair(0, 0)
+        gather_pair(0, 1)
+        low = maximum(0, 0, grouped_tile("xm0low", HALF_S))
+        high = maximum(0, HALF_S, grouped_tile("xm0high", HALF_S))
+        xm = quantise(low, "x0low") + quantise(high, "x0high")
         for jt in range(NODE_TILES):
-            copy = nc.vector.tensor_copy if jt == NODE_TILES - 1 else nc.scalar.copy
-            c_second = c_second + quantise(group_c(1, jt * P, P, copy), "c1_%d" % jt)
+            multiply_neighbours(jt, 0, xm[jt])
+
+        last = NODE_TILES - 1
+        late = grouped_tile("late", 3 * P)
+        gather_pair(1, 0)
+        gather_pair(1, 1)
+        low = maximum(1, 0, grouped_tile("xm1low", HALF_S))
+        third = maximum(1, HALF_S, grouped_tile("xm1third", P))
+        xm = quantise(low, "x1low")
+        maximum(1, last * P, late[:, 8 * P : 12 * P])
+        xm = xm + quantise(third, "x1third")
+        for jt in range(last):
+            multiply_neighbours(jt, 1, xm[jt])
+
+        c_first = quantise(group_c(0, 0, grouped_tile("c0low", HALF_S), nc.scalar.copy), "c0low")
+        group_c(0, HALF_S, late[:, 0 : 8 * P], nc.scalar.copy)
+        c_first = c_first + quantise(late[:, 0 : 4 * P], "c0third")
+        c_first_last, xm_last = quantise(late[:, 4 * P : 12 * P], "late")
+        c_first = c_first + [c_first_last]
+
+        c_second = quantise(group_c(1, 0, grouped_tile("c1_0", P), nc.scalar.copy), "c1_0")
+        last_grouped = group_c(1, last * P, margin_and_c[:, 0 : 2 * P].bitcast(BF16), nc.vector.tensor_copy)
+        for jt in range(1, last):
+            name = "c1_%d" % jt
+            c_second = c_second + quantise(group_c(1, jt * P, grouped_tile(name, P), nc.scalar.copy), name)
 
         for jt in range(NODE_TILES):
             multiply_own(jt, 0, c_first[jt])
+            if jt == last:
+                multiply_neighbours(jt, 1, xm_last)
             multiply_own(jt, 1, c_second[jt])
             store(jt)
+            if jt == 0:
+                c_second = c_second + quantise(last_grouped, "c1_last", tag="codes_c1_0")

@@ -79,9 +79,7 @@ def tile_list_sage_tm_none_kernel(tc, xT, c, w4_words, w4_scales, w8_words, w8_s
                 nc.sync.dma_start(rest[:, 1, columns], x_rows[a, :, 2 * u + 1, t0:t1])
                 x_raw[a, u, t0] = rest[:, :, columns]
 
-        c_first_raw = keep.tile([P, 4, S], F32, name="c_first_raw")
-        margin_and_c = keep.tile([P, P + 4 * S], F32, name="margin_and_c", align_bytes=64)
-        c_raw = [c_first_raw[:], margin_and_c[:, P : P + 4 * S].rearrange("p (i j) -> p i j", i=4)]
+        c_raw = [keep.tile([P, 4, S], F32, name="c_raw%d" % a)[:] for a in range(PASSES)]
 
         load_pair(0, 0)
         nc.sync.dma_start(offsets[:], offs)
@@ -92,7 +90,7 @@ def tile_list_sage_tm_none_kernel(tc, xT, c, w4_words, w4_scales, w8_words, w8_s
         nc.sync.dma_start(w4[:, 0].bitcast(I32), w4_words[0].bitcast(I32))
         nc.sync.dma_start(c_raw[0][:, 3], c_rows[0, :, 3])
         nc.sync.dma_start(w4[:, 1].bitcast(I32), w4_words[1].bitcast(I32))
-        nc.sync.dma_start(margin_and_c[:, P : P + 4 * S], c_rows[1].rearrange("p i j -> p (i j)"))
+        nc.sync.dma_start(c_raw[1], c_rows[1])
         for a in range(PASSES):
             nc.sync.dma_start(w8[:, a].bitcast(I32), w8_words[a].rearrange("p n i -> p (n i)").bitcast(I32))
 
@@ -204,10 +202,10 @@ def tile_list_sage_tm_none_kernel(tc, xT, c, w4_words, w4_scales, w8_words, w8_s
         c_first = c_first + [c_first_last]
 
         c_second = quantise(group_c(1, 0, grouped_tile("c1_0", P), nc.scalar.copy), "c1_0")
-        last_grouped = group_c(1, last * P, margin_and_c[:, 0 : 2 * P].bitcast(BF16), nc.vector.tensor_copy)
         for jt in range(1, last):
             name = "c1_%d" % jt
             c_second = c_second + quantise(group_c(1, jt * P, grouped_tile(name, P), nc.scalar.copy), name)
+        last_grouped = group_c(1, last * P, grouped_tile("c1_3", P), nc.scalar.copy)
 
         for jt in range(NODE_TILES):
             multiply_own(jt, 0, c_first[jt])

@@ -106,9 +106,10 @@ def tile_list_sage_tm_none_kernel(tc, xT, c, w4_words, w4_scales, w8_words, w8_s
                 rows = x_raw[a, u, t0]
                 scalar_columns = (t1 - t0) * sixths // 6 // (2 * RUN) * (2 * RUN)
                 split = t0 + scalar_columns
-                interleave(nc.scalar.copy, table[:, t0:split], rows[:, :, 0:scalar_columns])
+                by_column = rows.rearrange("p e t -> p t e")
+                nc.scalar.copy(table[:, t0:split], by_column[:, 0:scalar_columns])
                 if split < t1:
-                    interleave(nc.vector.tensor_copy, table[:, split:t1], rows[:, :, scalar_columns : t1 - t0])
+                    nc.vector.tensor_copy(table[:, split:t1], by_column[:, scalar_columns : t1 - t0])
             window = table[:].rearrange("p t e -> p (t e)").bitcast(U32)
             words = picked[a][:, u].rearrange("p g j -> p (g j)")
             cuts = [0, G * S - HALF_S, G * S] if u == 1 else [0, G * S]

from contextlib import ExitStack

import concourse.mybir as mybir

G, K, M, T, S = 2, 1024, 512, 2048, 512
FLOPS = 2 * 2 * K * M * S

F32 = mybir.dt.float32
BF16 = mybir.dt.bfloat16
I32 = mybir.dt.int32
U32 = mybir.dt.uint32
U16 = mybir.dt.uint16
U8 = mybir.dt.uint8
FP8X4 = mybir.dt.float8_e4m3fn_x4
FP4X4 = mybir.dt.float4_e2m1fn_x4

P = 128
PASSES = K // (4 * P)
NODE_TILES = S // P
HALF_S = S // 2
HALF_M = M // 2
RUN = 4

CHUNKS = {
    (0, 0): [(0, T // 2, 2), (T // 2, T, 2)],
    (0, 1): [(0, T // 2, 3), (T // 2, T, 2)],
    (1, 0): [(0, 3 * T // 8, 6), (3 * T // 8, T, 3)],
    (1, 1): [(0, 7 * T // 16, 6), (7 * T // 16, 3 * T // 4, 3), (3 * T // 4, T, 2)],
}


def tile_list_sage_tm_none_kernel(tc, xT, c, w4_words, w4_scales, w8_words, w8_scales, offs, out):
    nc = tc.nc
    with ExitStack() as ctx:
        keep = ctx.enter_context(tc.tile_pool(name="keep", bufs=1))
        psum = ctx.enter_context(tc.psum_pool(name="psum", bufs=1))

        offsets = keep.tile([P, G * S // 16], U16, name="offsets")

        w4 = keep.tile([P, PASSES, 2 * M], U8, name="w4", align_bytes=64)
        w8 = keep.tile([P, PASSES, M], U32, name="w8", align_bytes=64)

        s4 = keep.tile([P, PASSES, M], U8, name="s4", align_bytes=64)
        s8 = keep.tile([P, M], U8, name="s8", align_bytes=64)
        nc.vector.memset(s4[:].bitcast(I32), 0)
        nc.vector.memset(s8[:].bitcast(I32), 0)

        for q in range(4):
            nc.gpsimd.dma_start(
                s4[32 * q : 32 * q + 4].bitcast(I32),
                w4_scales[:, 4 * q : 4 * q + 4, :].rearrange("a r n -> r a n").bitcast(I32),
            )
        for q in range(4):
            nc.gpsimd.dma_start(
                s8[32 * q + 4 : 32 * q + 12].bitcast(I32), w8_scales[:, 4 * q : 4 * q + 4, :].bitcast(I32)
            )

        x_rows = xT.rearrange("(a p i) t -> a p i t", a=PASSES, i=4)
        c_rows = c.rearrange("(a p i) j -> a p i j", a=PASSES, i=4)
        x_raw = {}

        def load_pair(a, u):
            both = keep.tile([P, 2 * T], F32, name="x%d%d" % (a, u))
            source = x_rows[a, :, 2 * u : 2 * u + 2, :].rearrange("p e t -> p (e t)")
            for t0, t1, sixths in CHUNKS[a, u]:
                begin = T + t0 if t0 > 0 else 0
                nc.sync.dma_start(both[:, begin : T + t1], source[:, begin : T + t1])
                x_raw[a, u, t0] = both[:].rearrange("p (e t) -> p e t", e=2)[:, :, t0:t1]

        def load_last_pair(a, u):
            lead_end = CHUNKS[a, u][0][1]
            lead = keep.tile([P, 2, lead_end], F32, name="x_lead")
            rest = keep.tile([P, 2, T - lead_end], F32, name="x_rest")
            nc.sync.dma_start(lead[:], x_rows[a, :, 2 * u : 2 * u + 2, 0:lead_end])
            x_raw[a, u, 0] = lead[:]
            nc.sync.dma_start(rest[:, 0], x_rows[a, :, 2 * u, lead_end:T])
            for t0, t1, sixths in CHUNKS[a, u][1:]:
                columns = slice(t0 - lead_end, t1 - lead_end)
                nc.sync.dma_start(rest[:, 1, columns], x_rows[a, :, 2 * u + 1, t0:t1])
                x_raw[a, u, t0] = rest[:, :, columns]

        c_raw = [keep.tile([P, 4, S], F32, name="c_raw%d" % a)[:] for a in range(PASSES)]

        load_pair(0, 0)
        nc.sync.dma_start(offsets[:], offs)
        load_pair(0, 1)
        load_pair(1, 0)
        load_last_pair(1, 1)
        nc.sync.dma_start(c_raw[0][:, 0:3], c_rows[0, :, 0:3])
        nc.sync.dma_start(w4[:, 0].bitcast(I32), w4_words[0].bitcast(I32))
        nc.sync.dma_start(c_raw[0][:, 3], c_rows[0, :, 3])
        nc.sync.dma_start(w4[:, 1].bitcast(I32), w4_words[1].bitcast(I32))
        nc.sync.dma_start(c_raw[1], c_rows[1])
        for a in range(PASSES):
            nc.sync.dma_start(w8[:, a].bitcast(I32), w8_words[a].rearrange("p n i -> p (n i)").bitcast(I32))

        picked = [keep.tile([P, 2, G, S], U32, name="picked%d" % a) for a in range(PASSES)]
        acc = [[psum.tile([P, HALF_M], F32, name="acc%d%d" % (jt, h)) for h in range(2)] for jt in range(NODE_TILES)]

        def interleave(copy, grouped, rows):
            copy(grouped.rearrange("p (b t) e -> p b e t", t=RUN), rows.rearrange("p e (b t) -> p b e t", t=RUN))

        def gather_pair(a, u):
            table = keep.tile([P, T, 2], BF16, name="table%d%d" % (a, u))
            for t0, t1, sixths in CHUNKS[a, u]:
                rows = x_raw[a, u, t0]
                scalar_columns = (t1 - t0) * sixths // 6 // (2 * RUN) * (2 * RUN)
                split = t0 + scalar_columns
                by_column = rows.rearrange("p e t -> p t e")
                nc.scalar.copy(table[:, t0:split], by_column[:, 0:scalar_columns])
                if split < t1:
                    nc.vector.tensor_copy(table[:, split:t1], by_column[:, scalar_columns : t1 - t0])
            window = table[:].rearrange("p t e -> p (t e)").bitcast(U32)
            words = picked[a][:, u].rearrange("p g j -> p (g j)")
            cuts = [0, G * S - HALF_S, G * S] if u == 1 else [0, G * S]
            for m0, m1 in zip(cuts, cuts[1:]):
                nc.vector.tensor_copy(words[:, m0:m1], window.indirect(offsets[:, m0 // 16 : m1 // 16]))

        def grouped_tile(name, nodes):
            return keep.tile([P, 4 * nodes], BF16, name=name, align_bytes=64)[:]

        def maximum(a, j0, grouped):
            values = picked[a][:].bitcast(BF16).rearrange("p u g (j e) -> p g j u e", e=2)
            nodes = slice(j0, j0 + grouped.shape[1] // 4)
            nc.vector.tensor_tensor(
                grouped.rearrange("p (j u e) -> p j u e", u=2, e=2),
                values[:, 0, nodes],
                values[:, 1, nodes],
                mybir.AluOpType.max,
            )
            return grouped

        def group_c(a, j0, grouped, copy):
            width = grouped.shape[1] // 4
            interleave(copy, grouped.rearrange("p (j i) -> p j i", i=4), c_raw[a][:, :, j0 : j0 + width])
            return grouped

        def quantise(grouped, name, tag=""):
            width = grouped.shape[1] // 4
            codes = keep.tile([P, width], U32, name="codes_" + name, tag=tag, align_bytes=64)
            scales = keep.tile([P, width], U8, name="scales_" + name, align_bytes=64)
            nc.vector.quantize_mx(out=codes[:].bitcast(FP8X4), scales=scales[:], in_=grouped)
            return [(codes[:, b * P : (b + 1) * P], scales[:, b * P : (b + 1) * P]) for b in range(width // P)]

        def multiply_neighbours(jt, a, operand):
            codes, scales = operand
            for n0 in range(0, M, P):
                at = n0 % HALF_M
                nc.tensor.matmul_mx(
                    out=acc[jt][n0 // HALF_M][:, at : at + P],
                    lhsT=codes.bitcast(FP8X4),
                    lhsT_scale=scales,
                    rhs=w4[:, a, 2 * n0 : 2 * (n0 + P)].bitcast(FP4X4),
                    rhs_scale=s4[:, a, n0 : n0 + P],
                    start=a == 0 and at == 0,
                    stop=False,
                )

        def multiply_own(jt, a, operand):
            codes, scales = operand
            for h in range(2):
                columns = slice(h * HALF_M, (h + 1) * HALF_M)
                nc.tensor.matmul_mx(
                    out=acc[jt][h][:],
                    lhsT=codes.bitcast(FP8X4),
                    lhsT_scale=scales,
                    rhs=w8[:, a, columns].bitcast(FP8X4),
                    rhs_scale=s8[4 + 4 * a : P, columns],
                    start=False,
                    stop=a == PASSES - 1,
                )

        def store(jt):
            result = keep.tile([P, M], F32, name="result%d" % jt)
            nc.scalar.copy(result[:, 0:HALF_M], acc[jt][0][:])
            nc.vector.tensor_copy(result[:, HALF_M:M], acc[jt][1][:])
            nc.sync.dma_start(out[jt * P : (jt + 1) * P, :], result[:])

        gather_pair(0, 0)
        gather_pair(0, 1)
        low = maximum(0, 0, grouped_tile("xm0low", HALF_S))
        high = maximum(0, HALF_S, grouped_tile("xm0high", HALF_S))
        xm = quantise(low, "x0low") + quantise(high, "x0high")
        for jt in range(NODE_TILES):
            multiply_neighbours(jt, 0, xm[jt])

        last = NODE_TILES - 1
        late = grouped_tile("late", 3 * P)
        gather_pair(1, 0)
        gather_pair(1, 1)
        low = maximum(1, 0, grouped_tile("xm1low", HALF_S))
        third = maximum(1, HALF_S, grouped_tile("xm1third", P))
        xm = quantise(low, "x1low")
        maximum(1, last * P, late[:, 8 * P : 12 * P])
        xm = xm + quantise(third, "x1third")
        for jt in range(last):
            multiply_neighbours(jt, 1, xm[jt])

        c_first = quantise(group_c(0, 0, grouped_tile("c0low", HALF_S), nc.scalar.copy), "c0low")
        group_c(0, HALF_S, late[:, 0 : 8 * P], nc.scalar.copy)
        c_first = c_first + quantise(late[:, 0 : 4 * P], "c0third")
        c_first_last, xm_last = quantise(late[:, 4 * P : 12 * P], "late")
        c_first = c_first + [c_first_last]

        c_second = quantise(group_c(1, 0, grouped_tile("c1_0", P), nc.scalar.copy), "c1_0")
        for jt in range(1, last):
            name = "c1_%d" % jt
            c_second = c_second + quantise(group_c(1, jt * P, grouped_tile(name, P), nc.scalar.copy), name)
        last_grouped = group_c(1, last * P, grouped_tile("c1_3", P), nc.scalar.copy)

        for jt in range(NODE_TILES):
            multiply_own(jt, 0, c_first[jt])
            if jt == last:
                multiply_neighbours(jt, 1, xm_last)
            multiply_own(jt, 1, c_second[jt])
            store(jt)
            if jt == 0:
                c_second = c_second + quantise(last_grouped, "c1_last", tag="codes_c1_0")
